import numpy as np, ml_dtypes
CORES = [16,32,48,64,80]
N = 5
BF = ml_dtypes.bfloat16
H, H0, L, CAP, S, JS, T = 3072, 2816, 1280, 96, 3, 3, 3
TB = 4 * 2 ** JS
def edges(rng, late=False):
    nt = H // TB; m = H0 // TB; half = (m // 2) * TB; w = np.arange(H) // TB
    t = rng.integers(0, nt, (N, 8, nt))
    if late: t[:, :, :m // 2] = rng.integers(0, m, (N, 8, m // 2))
    base = t[:, :, w] * TB
    x = base + rng.integers(0, TB, (N, 8, H)); y = base + rng.integers(0, TB, (N, 8, H))
    odd = rng.random((N, 8, H)) < 0.1
    if late: odd = odd & (np.arange(H) >= half)
    return x, np.where(odd, rng.integers(0, H, (N, 8, H)), y)
def packets(rng, alive, pb):
    on = rng.random((N, 8, L)) < alive; j = rng.integers(0, 16, (N, 8, 1, L))
    live = on[:, :, None] & ((rng.random((N, 8, 16, L)) < np.broadcast_to(pb, (N, 8, L))[:, :, None]) | (np.arange(16)[:, None] == j))
    a = (1 + 0.5 * rng.random((N, 8, 16, L))) * (1 - 2 * rng.integers(0, 2, (N, 8, 16, L)))
    q = rng.choice(np.array([0.0, 0.15, 0.5, 0.5, 0.85, 1.0]), (N, 8, 1, L))
    c = rng.random((N, 8, 16, L)) * np.where(rng.random((N, 8, 16, L)) < q, 1.0, -1.0)
    return live, a, c, rng.integers(0, H, (N, 8, L))
def pack(rng, live, a, c, h, x, y, kap=None, dam=None):
    if kap is None: kap = 0.5 + 0.5 * rng.random((N, 128, H), dtype=np.float32)
    if dam is None: dam = 1.5 + 2.5 * rng.random((N, 128, H), dtype=np.float32)
    c = np.where(np.abs(c) < 2.0 ** -20, 0.0 * c, c)
    return {"kap": kap.astype(BF), "dam": dam.astype(BF), "lf": x.astype(np.int32), "rt": y.astype(np.int32), "place": h.astype(np.int32),
            "cro": c.reshape(N, 128, L).astype(BF), "amp": np.where(live, np.abs(a), 0.0 * a).reshape(N, 128, L).astype(BF)}
def ends(rng, v, share):
    return np.where(rng.random(v.shape) < share, (H - 1) * rng.integers(0, 2, v.shape), v)
def setup_inputs(rng):
    x, y = edges(rng)
    alive = rng.permuted(np.tile(np.array([0.08, 0.12, 0.2, 0.25, 0.35, 0.45, 0.5, 0.6]), (N, 1)), axis=1)[:, :, None]
    live, a, c, h = packets(rng, alive, rng.choice(np.array([0.5, 0.8, 1.0]), (N, 8, L)))
    return pack(rng, live, a, c, h, x, y)
def setup_inputs_calm(rng):
    x, y = edges(rng); live, a, c, h = packets(rng, 0.6, 0.9); o = int(rng.integers(0, 8))
    for r in range(N):
        for k in range(5):
            g = (o + k) % 8
            x[r, g] = np.where(rng.random(H) < 0.002, rng.integers(H0, H, H), x[r, g] % H0); y[r, g] = np.where(rng.random(H) < 0.002, rng.integers(H0, H, H), y[r, g] % H0)
            live[r, g] = np.arange(16)[:, None] == rng.integers(0, 16, L)
            p = rng.permutation(L); h[r, g] = rng.integers(0, H0, L)
            two = p[:4]; live[r, g][:, two] = False
            for l in two:
                b = rng.permutation(16)[:2]; live[r, g, b, l] = True; c[r, g, b[0], l] = 0.5; c[r, g, b[1], l] = -0.5
            nd = (r + k) % 4; h[r, g, p[4:4 + nd]] = rng.integers(H0, H, nd)
            nf = (k + 2 * r + 1) % 4; live[r, g][:, p[8:8 + nf]] = False
    return pack(rng, live, a, c, h, x, y)
def setup_inputs_corners(rng):
    x, y = edges(rng, True); live, a, c, h = packets(rng, 1.0, 0.9); half = (H0 // TB // 2) * TB; n2 = (H - H0) // 2
    g0 = int(rng.integers(0, 8)); cell = {}
    for j in range(4):
        g = (g0 + (0, 4, 2, 6)[j]) % 8
        cell[0, g] = ((L - 2 * CAP, L - 2 * CAP + 1, (L - 2 * CAP) // 2, 0)[j], 0, 0)
        cell[N - 1, g] = (L // 2, (CAP + 1, L // 2, L // 2, 0)[j], 0)
        cell[N - S, (g - 1) % 8] = (L // 2, (CAP + 2, L // 2, L // 2, 0)[j], 1)
    for r in range(N):
        for g in range(8):
            n = (0, 1, L, L - 1, L - 2, L - 3, L // 2, L // 4)[(r + g) % 8]; v = (3 * r + g) % 8
            k = min(n, (CAP, CAP + 1, 1, 0, L, CAP - 1, 2, 3)[v]); odd = {0: 0, 1: 0, 5: 1}.get(v)
            if (r, g) in cell: n, k, odd = cell[r, g]
            p = rng.permutation(L)[:n] if n != 1 else np.array([L - 1])
            keep = np.zeros(L, bool); keep[p] = True; live[r, g] &= keep
            if (r, g) in cell and k == 0: live[r, g] = keep & (np.arange(16)[:, None] == rng.integers(0, 16, L))
            h[r, g] = rng.integers(0, half, L)
            par = rng.integers(0, 2, k) if odd is None else np.full(k, odd)
            h[r, g, p[:k]] = H0 + 2 * rng.integers(0, n2, k) + par
    g = (g0 + 2) % 8; o = rng.permutation(half); p, s, u = int(o[0]), int(o[1]), int(o[2])
    x[0, g, p] = s; x[0, g, s] = u; y[0, g, s] = (u + 2 ** JS) % half
    l = np.flatnonzero(np.any(live[0, g], axis=0)); b = rng.integers(0, 16, len(l)); b2 = (b + rng.integers(1, 16, len(l))) % 16
    live[0, g] = False; live[0, g, b, l] = True; live[0, g, b2, l] = True; h[0, g] = p
    c[0, g, b, l] = 1.0; c[0, g, b2, l] = 0.125 + 0.25 * rng.random(len(l))
    g = (g0 + 6) % 8
    for r, k, odd in ((N - 1, g, 0), (N - S, (g - 1) % 8, 1)):
        o = rng.permutation(half); p, s = int(o[0]), int(o[1]); door = H0 + 2 * int(rng.integers(0, n2)) + odd
        h[r, k] = p; x[r, k, p] = s; y[r, k, p] = s; x[r, k, s] = door; y[r, k, s] = door
    return pack(rng, live, a, c, h, x, y)
def setup_inputs_crowd(rng):
    x, y = edges(rng); live, a, c, h = packets(rng, 0.5, 1.0); i = (np.arange(16)[:, None] + np.arange(L)) % 16
    for r in range(N):
        for g in range(8):
            u = (r + g) % 8
            if u == 7: continue
            p = int(rng.integers(0, H0)); door = int(rng.integers(H0, H))
            h[r, g] = door if u in (3, 4) else p
            if u in (0, 1, 3, 4): live[r, g] = True
            if u in (1, 4): live[r, g][:, int(rng.integers(0, L))] = False
            if u == 4: h[r, g, int(rng.integers(0, L))] = p
            left = (16, 15, 8, 16, 1, 8, 7)[u]
            c[r, g] = np.abs(c[r, g]) * np.where(i < left, 1.0, -1.0)
            j = int(rng.integers(0, H0 // TB)) * TB
            if u in (0, 1, 2, 5, 6): x[r, g, p] = j; y[r, g, p] = j + (2 ** JS - 1 if u == 2 else 2 ** JS)
    g = int(rng.integers(0, 8)); e = 2 * int(rng.integers(0, (H - H0) // 2)); o = rng.permutation(H0); p = int(o[0]); s = int(o[1])
    live[N - 1, g] = True; h[N - 1, g] = H0 + e
    m = (e >> JS << JS) + rng.integers(0, 2 ** JS, 2)
    x[0, g, p] = s; y[0, g, p] = int(rng.integers(H0, H)); x[0, g, s] = m[0]; y[0, g, s] = m[1]
    l = rng.permutation(L)[:CAP]; b = rng.integers(0, 16, CAP); b2 = (b + rng.integers(1, 16, CAP)) % 16
    live[0, g] = False; live[0, g, b, l] = True; live[0, g, b2, l] = True; h[0, g] = p
    c[0, g, b, l] = 0.25 + 0.5 * rng.random(CAP); c[0, g, b2, l] = -0.25 - 0.5 * rng.random(CAP)
    return pack(rng, live, a, c, h, x, y)
def setup_inputs_ends(rng):
    x, y = edges(rng); x = ends(rng, x, 0.8); y = ends(rng, y, 0.8); k = (np.arange(N)[:, None] + np.arange(8)) % 4
    x[:, :, 0] = np.array([0, H - 1, 0, H0 - 1])[k]; y[:, :, 0] = np.array([H - 1, 0, 0, H - 1])[k]
    x[:, :, H - H0 - 1] = 0; y[:, :, H - H0 - 1] = H - 1; x[:, :, H - 1] = 0; y[:, :, H - 1] = H - 1
    live, a, c, h = packets(rng, 0.5, rng.integers(0, 2, (N, 8, L)).astype(np.float64)); h = ends(rng, h, 0.8)
    big = rng.random(a.shape) < rng.choice(np.array([0.0, 0.5, 1.0]), (N, 8, 1, L))
    a = np.where(a < 0, -1.0, 1.0) * np.where(big, 4.0, 0.25)
    e = rng.choice(np.array([-1.0, -2.0 ** -20, -0.0, 0.0, 2.0 ** -20, 1.0]), c.shape); c = np.where(rng.random(c.shape) < 0.7, e, c)
    h[:, :, 0] = 0; h[:, :, L - 1] = H - 1; h[N - 1, 7, L - 1] = 0; h[0, :4, L - 1] = 0
    tie = np.where(np.arange(16) < 8, 2.0 ** -20, -2.0 ** -20)
    for l in (0, L - 1): live[:, :, :, l] = True; c[:, :, :, l] = tie
    return pack(rng, live, a, c, h, x, y, np.where(rng.random((N, 128, H)) < 0.5, 0.5, 1.0), np.where(rng.random((N, 128, H)) < 0.25, 0.0, 4.0))
def setup_inputs_spread(rng):
    x, y = edges(rng); live, a, c, h = packets(rng, 0.5, 0.95)
    a = a * np.exp2(rng.integers(-1, 2, (N, 8, 1, L))); h = np.minimum((H * rng.random((N, 8, L)) ** 2).astype(np.int64), H - 1)
    low = rng.random((N, 1, H)) < 0.25
    dam = np.where(low, 1.4 * rng.random((N, 1, H)), 1.5 + 2 * rng.random((N, 1, H))) + 0.5 * rng.random((N, 128, H))
    kap = 0.5 + 0.5 * rng.random((N, 128, H), dtype=np.float32); i = np.arange(16) % 2
    for r in range(N):
        g = int(rng.integers(0, 8)); o = rng.permutation(H0); p, s, v = int(o[0]), int(o[1]), int(o[2]); l = rng.permutation(L)[:32]
        kap[r, 16 * g:16 * g + 16, p] = np.where(i == 0, 155, 205) * 2.0 ** -8; kap[r, 16 * g:16 * g + 16, s] = 132 * 2.0 ** -8
        x[r, g, p] = s; y[r, g, s] = v; h[r, g, l] = p
        live[r, g][:, l] = True; c[r, g][:, l] = (np.where(i == 0, 205, 155) * 2.0 ** -13)[:, None]
    return pack(rng, live, a, c, h, x, y, kap, dam)
def check_ranges(d):
    bad = []
    for k, lo, hi in (("lf", 0, H - 1), ("rt", 0, H - 1), ("place", 0, H - 1), ("kap", 0.5, 1.0), ("dam", 0.0, 4.0)):
        v = np.asarray(d[k], np.float64)
        if not (np.min(v) >= lo and np.max(v) <= hi): bad.append("range of " + k)
    for k, lo, hi in (("cro", 2.0 ** -20, 1.0), ("amp", 0.25, 4.0)):
        v = np.asarray(d[k], np.float64)
        if k == "cro": v = np.abs(v)
        if not np.all((v == 0) | ((v >= lo) & (v <= hi))): bad.append("range of " + k)
    return bad
def at(t, ix):
    return np.take_along_axis(t, ix, t.ndim - 1)
def reference(kap, dam, lf, rt, place, cro, amp):
    kf = kap.astype(np.float32).reshape(N, 8, 16, H)
    sg = np.reciprocal(1.0 + np.exp(-dam.astype(np.float64))).reshape(N, 8, 16, H)
    xt = lf.astype(np.int64); yt = rt.astype(np.int64); h = place.astype(np.int64)
    a = amp.astype(np.float64).reshape(N, 8, 16, L); one = np.float32(1); nil = np.float32(0)
    c = np.where(a != 0, cro.astype(np.float32).reshape(N, 8, 16, L), nil)
    own = np.arange(L); tw = np.tile(own, (N, 8, 1)); box = {}
    for step in range(T):
        live = a != 0; on = np.any(live, axis=2); go = on & (h < H0); moves = live & go[:, :, None]
        k = at(kf, h[:, :, None]) * c
        left = moves & (k >= 0); right = moves & (k < 0); k = np.float32(2) * k
        c = np.where(left, k - one, np.where(right, k + one, c))
        xl = at(xt, h); xr = at(yt, h)
        a = np.where(left, a * at(sg, xl[:, :, None]), np.where(right, a * at(sg, xr[:, :, None]), a))
        lw = np.sum(left, axis=2) >= np.sum(right, axis=2)
        out = np.where(lw[:, :, None], right, left); dis = np.any(out, axis=2)
        h = np.where(go, np.where(lw, xl, xr), h); other = np.where(lw, xr, xl)
        da = np.where(out, a, 0.0); dc = np.where(out, c, nil)
        a = np.where(out, 0.0, a); c = np.where(out, nil, c)
        for r in range(N):
            for g in range(8):
                w = np.flatnonzero(~on[r, g]); d = np.flatnonzero(dis[r, g])
                nh = [other[r, g, d]]; na = [da[r, g][:, d]]; nc = [dc[r, g][:, d]]; m = 0
                if step > 0:
                    e0, a0, c0 = box[(r - 1) % N, g]; e1, a1, c1 = box[(r - S) % N, (g - 1) % 8]
                    i0 = e0 % 2 == 0; i1 = e1 % 2 == 1
                    nh = [e0[i0], e1[i1]] + nh; na = [a0[:, i0], a1[:, i1]] + na; nc = [c0[:, i0], c1[:, i1]] + nc
                    m = len(nh[0]) + len(nh[1])
                nh = np.concatenate(nh); na = np.concatenate(na, axis=1); nc = np.concatenate(nc, axis=1)
                n = min(len(w), len(nh)); w = w[:n]
                h[r, g, w] = nh[:n]; a[r, g][:, w] = na[:, :n]; c[r, g][:, w] = nc[:, :n]
                tw[r, g, w[:m]] = w[:m]; born = w[m:]; par = d[:len(born)]
                tw[r, g, born] = par; tw[r, g, par] = born
        on = np.any(a != 0, axis=2)
        f = on & at(on, tw) & (at(tw, tw) == own) & (tw != own) & ((h >> JS) == (at(h, tw) >> JS))
        lo = (f & (own < tw))[:, :, None]; up = (f & (own > tw))[:, :, None]; ix = tw[:, :, None]
        a = np.where(lo, a + at(a, ix), np.where(up, 0.0, a)); c = np.where(lo, c + at(c, ix), np.where(up, nil, c))
        if step < T - 1:
            on = np.any(a != 0, axis=2)
            for r in range(N):
                for g in range(8):
                    e = np.flatnonzero(on[r, g] & (h[r, g] >= H0))[:CAP]
                    box[r, g] = (h[r, g, e] - H0, a[r, g][:, e], c[r, g][:, e])
                    a[r, g][:, e] = 0.0; c[r, g][:, e] = nil
    y = a * at(kf, h[:, :, None])
    return {"ya": y.reshape(N, 128, L).astype(np.float32), "yc": c.reshape(N, 128, L).astype(np.float32)}

def check_inputs(d):
    bad = list(check_ranges(d))
    if not bad:
        for name, y in reference(**d).items():
            for q in range(N):
                v = np.abs(np.asarray(y[q], np.float64)); s = np.sqrt(np.mean(v * v))
                if v.max() > 7 * s or s < 2.0 ** -4: bad.append('%s of rank %d is uneven or too small' % (name, q))
    return bad

@@ -1,0 +1,649 @@
+from concourse.bass import DstId, RemoteDMATransfer
+from concourse.mybir import AluOpType as A, ActivationFunctionType as F
+
+L, H, H0 = 1280, 3072, 2816
+OU, OA_, OL, OR, OARR, DEAD, OB, NY = 0, 1280, 2560, 3840, 5120, 5504, 5520, 6800
+XF, XP, XD, NX = 1280, 2560, 3312, 3520
+CH = [(0, 448), (448, 864), (864, 1280)]
+NW, NB, NU, NI = 10240, 9216, 768, 1536
+
+SCRATCH = {
+    "kt": ("sbuf", [128, 3328], "bfloat16"), "dt": ("sbuf", [128, H], "bfloat16"), "tab": ("sbuf", [128, H], "bfloat16"),
+    "ycw": ("sbuf", [128, NY], "float32"), "yaw": ("sbuf", [128, NY], "float32"),
+    "idc": ("sbuf", [128, 1664], "bfloat16"), "xw": ("sbuf", [128, NX], "bfloat16"), "ones": ("sbuf", [128, 512], "bfloat16"),
+    "w": ("sbuf", [128, NW], "float32"), "wb": ("sbuf", [128, NB], "bfloat16"),
+    "wu": ("sbuf", [128, NU], "uint16"), "wi": ("sbuf", [128, NI], "int32"),
+}
+for _n in ("crb", "amb", "rr", "dd", "gx", "dl", "dr", "pb", "xg"):
+    SCRATCH[_n] = ("sbuf", [128, L], "bfloat16")
+for _n in ("cp", "g2c", "g2a", "oc", "oa"):
+    SCRATCH[_n] = ("sbuf", [128, L], "float32")
+for _n in ("1", "2"):
+    SCRATCH["sh" + _n] = ("sbuf", [128, 96], "bfloat16")
+    SCRATCH["lh" + _n] = ("sbuf", [128, 192], "bfloat16")
+    SCRATCH["sd" + _n] = ("sbuf", [128, 192], "float32")
+    SCRATCH["ld" + _n] = ("sbuf", [128, 384], "float32")
+for _b in range(8):
+    SCRATCH["p%d" % _b] = ("psum", [128, 512], "float32")
+SCRATCH["vl"] = ("sbuf", [128, 3 * L], "bfloat16")
+NDMA = 44
+SEMAPHORES = ["sv", "ss", "sp", "sg", "sent", "rh1", "rh2", "rd1", "rd2"] + ["d%d" % _i for _i in range(NDMA)]
+TWO = [_n for _n in SCRATCH if SCRATCH[_n][2] in ("bfloat16", "uint16")]
+CY = 0.83e-3 * 1.25
+GC, SC, LAT, NET, OV = 1.56, 3.8, 0.1, 3.0, 0.02
+PC, DM = 0.52e-3, 1.0
+OPT = {"XS": (640, 640, 960), "CV": (0,), "DV": (), "GV": (1,), "VS": ((1, 0), (1, 1), (2, 0), (2, 1), (3, 0), (3, 1)),
+       "PV": (), "KP": (0, 1), "AL": 0.05, "IT": 8, "SEED": 764, "NZ": 0.3}
+KEPT = {}
+
+
+def rank_program(g, core, T, topo):
+    rank = T.rank_of(core)
+    if rank is None:
+        return
+    nr = len(T.cores)
+    ops, acc, top, names = [], {}, {"w": 0, "wb": 0, "wu": 0, "wi": 0}, {}
+
+    def v(name, a, b, s=1):
+        return (name, a, b, s)
+
+    def new(buf, n=80):
+        a = top[buf]
+        top[buf] = a + (n + 15) // 16 * 16
+        assert top[buf] <= SCRATCH[buf][1][1]
+        return (buf, a, a + n, 1)
+
+    def sub(x, a, b, s=1):
+        return (x[0], x[1] + a, x[1] + b, s)
+
+    def ind(win, off):
+        return ("ind", win, off)
+
+    def ap(x):
+        if not isinstance(x, tuple):
+            return x
+        if x[0] == "ind":
+            return ap(x[1]).indirect(ap(x[2]))
+        return T[x[0]][:, x[1]:x[2]] if x[3] == 1 else T[x[0]][:, x[1]:x[2]:x[3]]
+
+    def cnt(x):
+        return 16 * cnt(x[2]) if x[0] == "ind" else (x[2] - x[1] + x[3] - 1) // x[3]
+
+    def psum(x):
+        return x[0][0] == "p" and x[0][1:].isdigit()
+
+    def op(eng, fn, R, W, cost, hold=None, sem=None, xw=None, after=None):
+        rs, ws = [], []
+        for x in R:
+            if isinstance(x, tuple):
+                rs += [x[1], x[2]] if x[0] == "ind" else [x]
+        for x in W:
+            if x[0] == "ind":
+                ws.append(x[1])
+                rs.append(x[2])
+            else:
+                ws.append(x)
+        me, deps = len(ops), set()
+        for x, w in [(x, False) for x in rs] + [(x, True) for x in ws]:
+            ps = psum(x)
+            for (j, a, b, w2, e2) in acc.setdefault(x[0], []):
+                if (ps and e2 != eng) or ((w or w2) and a < x[2] and x[1] < b):
+                    deps.add(j)
+        for x, w in [(x, False) for x in rs] + [(x, True) for x in ws]:
+            acc[x[0]].append((me, x[1], x[2], w, eng))
+        ops.append({"e": eng, "fn": fn, "deps": deps, "cost": cost, "hold": cost if hold is None else hold, "sem": sem,
+                    "xw": xw, "after": after})
+        return me
+
+    def vcost(o, xs, two=False):
+        n = cnt(o)
+        if o[0] == "ind":
+            return 0.05 + n * SC * CY
+        if any(isinstance(x, tuple) and x[0] == "ind" for x in xs):
+            return 0.05 + n * GC * CY
+        if two:
+            f = 1.0 if any(psum(x) for x in xs) else 2.0
+        else:
+            f = 0.5 if o[0] in TWO and xs[0][0] in TWO else 1.0
+        return OV + max(64, n * f) * CY
+
+    def tt(o, a, b, f):
+        op("v", lambda: g.vector.tensor_tensor(ap(o), ap(a), ap(b), f), [a, b], [o], vcost(o, [a, b], True))
+        return o
+
+    def ts(o, a, s1, f1, s2=None, f2=None):
+        if f2 is None:
+            fn = lambda: g.vector.tensor_scalar(ap(o), ap(a), ap(s1), None, f1)
+        else:
+            fn = lambda: g.vector.tensor_scalar(ap(o), ap(a), ap(s1), ap(s2), f1, f2)
+        op("v", fn, [a, s1, s2], [o], vcost(o, [a]))
+        return o
+
+    def cp(o, a):
+        op("v", lambda: g.vector.tensor_copy(ap(o), ap(a)), [a], [o], vcost(o, [a]))
+        return o
+
+    def fill(o, c):
+        op("v", lambda: g.vector.memset(ap(o), c), [], [o], OV + max(64, cnt(o) * (0.5 if o[0] in TWO else 1)) * CY)
+        return o
+
+    def scan(o, a):
+        one = v("ones", 0, cnt(a))
+        op("v", lambda: g.vector.tensor_tensor_scan(ap(o), ap(one), ap(a), 0.0, A.mult, A.add), [a, one], [o], vcost(o, [a]))
+        return o
+
+    def act(o, a, f, scale=1.0, bias=None, accum=None, extra=(), xw=None, after=None):
+        kw = {"scale": ap(scale)}
+        if bias is not None:
+            kw["bias"] = ap(bias)
+        if accum is not None:
+            kw["accum_out"] = ap(accum)
+        c = 0.065 + cnt(o) * GC * CY if a[0] == "ind" else OV + max(64, cnt(o)) * CY + (0.02 if accum else 0)
+        op("s", lambda: g.scalar.activation(ap(o), ap(a), f, **kw), [a, scale, bias] + list(extra),
+           [o] + ([accum] if accum else []), c, xw=xw, after=after)
+        return o
+
+    def lin(o, a, scale, bias):
+        return act(o, a, F.Identity, scale, bias)
+
+    def pe(items, wide=1, xw=None, after=None):
+        def fn():
+            last = None
+            for (o, l, r, st, sp) in items:
+                last = g.tensor.matmul(ap(o), ap(l), ap(r), st, sp)
+            return last
+        op("p", fn, [x[1] for x in items] + [x[2] for x in items], [x[0] for x in items],
+           0.05 + sum(max(64, cnt(x[2])) * wide * PC for x in items), xw=xw, after=after)
+
+    def conv(o, B, src):
+        n = cnt(src)
+        pe([(o, sub(B, 15 - i, 143 - i), sub(src, i, n, 16), i == 0, i == 15) for i in range(16)])
+        return o
+
+    def iota(o, pat, base, mul):
+        if o[0] == "wi":
+            fn = lambda: g.iota(ap(o), pat, base, mul)
+        else:
+            fn = lambda: g.iota(ap(o), pat, base, mul, allow_small_or_imprecise_dtypes=True)
+        op("g", fn, [], [o], 0.13 + 2 * cnt(o) * CY)
+        return o
+
+    nd = [0]
+
+    def dma(eng, out, in_, R, W, cost, add=False):
+        q = {"y": g.sync, "s": g.scalar, "g": g}[eng]
+        s = "d%d" % nd[0]
+        nd[0] += 1
+        kw = {"accum_op": A.add} if add else {}
+        op(eng, lambda: q.dma_start(out, in_, **kw), R, W, cost * DM, hold=0.6 * DM if eng == "g" else 0.1, sem=s)
+
+    def dsum(o, a, b):
+        dma("y", ap(o), ap(a), [a], [o], 3.2)
+        dma("g", ap(o), ap(b), [b, o], [o], 4.5, True)
+
+    def send(src, land, n, sem):
+        trs = []
+        for k, step in enumerate((1, 3)):
+            dst = T.cores[(rank + step) % nr]
+            rid, pid = topo.addr(dst)[:2]
+            eng = topo.engines(core, dst)
+            half = len(eng) // 2
+            m = sum(1 << e for e in eng[k * half:(k + 1) * half])
+            trs.append(RemoteDMATransfer(dst_ids=[DstId(rid=rid, pnc=pid)], dma_engine_mask=m, remote_sem=T.sem[sem],
+                                         src=T[src][:], dst=T[land][:, k * n:(k + 1) * n]))
+            names["sent"] = names.get("sent", 0) + half
+            names[sem] = names.get(sem, 0) + half
+        return op("g", lambda: g.remote_dma_fused(trs, local_sem=T.sem.sent), [v(src, 0, n)], [], 0.5, sem="none")
+
+    W = lambda n=80: new("w", n)
+    Bf = lambda n=80: new("wb", n)
+    U = lambda n=80: new("wu", n)
+    I32 = lambda n=80: new("wi", n)
+    P = lambda b, a, c: v("p%d" % b, a, c)
+    Q = lambda k, n=80: v("p7", 80 * k, 80 * k + n)
+    lst = lambda x, a, b: sub(x, a // 16, b // 16)
+
+    pli, exi = I32(80), I32(352)
+    dma("s", ap(sub(exi, 0, 176)), T.lf[:, 0:H0], [], [sub(exi, 0, 176)], 2.0)
+    dma("y", ap(sub(exi, 176, 352)), T.rt[:, 0:H0], [], [sub(exi, 176, 352)], 2.0)
+    dma("s", ap(pli), T.place[:], [], [pli], 2.0)
+    dma("y", T.amb[:], T.amp[:], [], [v("amb", 0, L)], 2.4)
+    dma("y", T.crb[:], T.cro[:], [], [v("crb", 0, L)], 2.8)
+    dma("y", T.kt[:, 0:H0], T.kap[:, 0:H0], [v("crb", 0, 1)], [v("kt", 0, H0)], 3.2)
+    dma("y", T.dt[:], T.dam[:], [v("crb", 0, 1)], [v("dt", 0, H)], 4.4)
+    dma("y", T.kt[:, H:H + 256], T.kap[:, H0:H], [v("crb", 0, 1)], [v("kt", H, H + 256)], 4.5)
+
+    pi = iota(I32(1), [[0, 1]], 0, 1)
+    xrow = iota(W(144), [[1, 144]], -15, 0)
+    g16 = iota(W(128), [[16, 8], [0, 16]], 0, 0)
+    ownp = iota(W(80), [[16, 80]], 0, 1)
+    dhi = iota(W(256), [[1, 4], [0, 64]], H0 // 64, 0)
+    dlo = iota(W(256), [[0, 4], [1, 64]], 0, 0)
+    ida = iota(Bf(416), [[1, 26], [0, 16]], 0, 0)
+    idb = iota(Bf(416), [[0, 26], [1, 16]], 0, 0)
+    dma("g", T.yaw[:, OA_:OA_ + L], T.amp[:], [idb, v("kt", 0, 1)], [v("yaw", OA_, OA_ + L)], 4.0)
+    fill(v("xw", 0, 704), 0.0)
+    fill(v("tab", 0, 1408), 0.0)
+    dma("s", T.tab[:, 1408:H0], T.tab[:, 0:1408], [v("tab", 0, 1408)], [v("tab", 1408, H0)], 2.4)
+    fill(v("ones", 0, 512), 1.0)
+    fill(v("kt", H0, H), 0.5)
+    for k in range(1, 5):
+        dma("y", T.xw[:, 704 * k:704 * k + 704], T.xw[:, 0:704], [v("xw", 0, 704), v("crb", 0, 1)], [v("xw", 704 * k, 704 * k + 704)], 3.0)
+    pf = cp(W(1), pi)
+    pm = cp(W(1), ts(I32(1), pi, 15, A.bitwise_and))
+    t16 = ts(I32(1), pi, 16, A.bitwise_and)
+    me_ = ts(W(1), t16, 0.0, A.is_equal)
+    mo_ = ts(W(1), t16, 0.0, A.is_gt)
+    pg = tt(W(1), pf, pm, A.subtract)
+    mrow, j1 = sub(xrow, 15, 143), sub(xrow, 16, 112)
+    oh = ts(W(16), sub(xrow, 15, 31), pm, A.is_equal)
+    OH = lambda j: sub(oh, j, j + 1)
+    B0 = ts(Bf(144), xrow, pg, A.is_equal)
+    own = ts(W(), ownp, pg, A.subtract)
+    ONES = ts(Bf(128), g16, pg, A.is_equal)
+    IDN = ts(Bf(128), mrow, pf, A.is_equal)
+    NUT = tt(Bf(128), ts(Q(0, 128), mrow, pf, A.is_le, -1.0, A.mult), ONES, A.mult)
+
+    def col(terms, c=None):
+        for j, wgt in terms:
+            c = act(W(1), OH(j), F.Identity, float(wgt), c)
+        return c
+
+    def scaled(src, c):
+        return act(Bf(cnt(src)), src, F.Copy, c)
+
+    wxl, wxr = col([(0, 64), (4, 1)]), col([(8, 64), (12, 1)])
+    Bxl, Bxr, Bdf = scaled(B0, wxl), scaled(B0, wxr), scaled(B0, lin(W(1), wxl, -1.0, wxr))
+    Bid = scaled(B0, col([(2, 16), (3, 1), (6, 2048)]))
+    wv = col([(5, -1280), (7, 1280)])
+    Bw = {k: scaled(B0, col([(1, k)], wv)) for k in (OA_ - OL, OB - OL)}
+    Bsix, Bpm = scaled(B0, 0.0625), scaled(B0, pm)
+    O16 = scaled(ONES, 0.0625)
+    M57 = tt(Bf(128), sub(B0, 10, 138), sub(B0, 8, 136), A.add)
+    Mrr, Mdd = scaled(M57, -1.0), scaled(M57, -0.5)
+    MG = tt(Bf(128), ts(Q(2, 128), M57, OH(1), A.mult, 64.0, A.mult), IDN, A.add)
+    I2048n, I64p, I64n = [scaled(IDN, c) for c in (-2048.0, 64.0, -64.0)]
+    vb = {True: OH(5), False: col([(5, -7), (7, -8)])}
+    B32, M64 = scaled(B0, 1.0 / 32), scaled(M57, -1.0 / 64)
+    mhi, mlo = col([(0, 1), (8, 1)]), col([(4, 1), (12, 1)])
+    nmlo = act(W(1), mlo, F.Copy, -1.0)
+    jb = lin(W(6), sub(own, 0, 6), -1.0, -0.5)
+    ownm = lin(W(), own, 1.0, -float(XF))
+    co1, co2 = lin(W(), own, 1.0, float(OR - DEAD)), lin(W(), own, 1.0, float(OL - DEAD))
+    pgn0 = lin(W(1), pg, 1.0, 16.0)
+    pgn = tt(W(1), pgn0, ts(W(1), pgn0, 128.0, A.is_ge, 128.0, A.mult), A.subtract)
+    SHO = ts(Bf(128), g16, pgn, A.is_equal, -1.0, A.mult)
+    SHF = ts(W(128), mrow, lin(W(1), pgn, 1.0, pm), A.is_equal)
+    cs1 = lin(W(12), sub(own, 0, 12), -1.0, float(XP - 1 - XD))
+    cs2 = lin(W(12), sub(own, 0, 12), 1.0, float(XD))
+    kk = W(160)
+    lin(sub(kk, 0, 80), own, -1.0, float(XP + 2048))
+
+    for k in range(4):
+        a, b = 416 * k, 416 * k + 416
+        if k == 0:
+            pe([(P(0, 0, 416), sub(Bsix, 13, 141), ida, True, False), (P(0, 0, 416), sub(Bsix, 12, 140), idb, False, True)])
+            act(v("idc", a, b), P(0, 0, 416), F.Copy)
+        else:
+            ts(v("idc", a, b), v("idc", 0, 416), col([(2, 26 * k)]), A.add)
+
+    hl, hlb = I32(704), Bf(704)
+    cp(sub(hlb, 0, 352), ts(sub(hl, 0, 352), exi, 6, A.arith_shift_right))
+    cp(sub(hlb, 352, 704), ts(sub(hl, 352, 704), exi, 63, A.bitwise_and))
+    for row, a, e in ((0, 0, "y"), (8, 176, "s"), (4, 352, "y"), (12, 528, "s")):
+        dma(e, T.tab[row:128:16, 0:H0], ap(sub(hlb, a, a + 176)), [sub(hlb, a, a + 176), v("tab", 0, H0)],
+            [v("tabrow%d" % row, 0, 1)], 2.5)
+    tt(v("tab", H0, H), lin(P(4, 0, 256), dhi, mhi, OH(1)), act(W(256), dlo, F.Copy, mlo), A.add)
+    tabr = [v("tabrow%d" % r, 0, 1) for r in (0, 4, 8, 12)]
+
+    plf, pin, pout, h = cp(W(), pli), W(160), W(160), W()
+    for u in range(5):
+        ts(sub(pin, 32 * u, 32 * u + 16), sub(plf, 16 * u, 16 * u + 16), me_, A.mult)
+        act(sub(pin, 32 * u + 16, 32 * u + 32), sub(plf, 16 * u, 16 * u + 16), F.Copy, mo_)
+    op("v", lambda: g.vector.transpose(ap(pout), ap(pin)), [pin], [pout], 0.19)
+    for u in range(5):
+        tt(sub(h, u, 80, 5), sub(pout, 32 * u, 32 * u + 16), sub(pout, 32 * u + 16, 32 * u + 32), A.add)
+
+    ts(v("dd", 0, L), v("amb", 0, L), 0.0, A.is_equal, 64.0, A.mult)
+    dma("g", T.cp[:], T.cro[:], [dlo], [v("cp", 0, L)], 4.0)
+    dma("g", T.cp[:], T.dd[:], [v("dd", 0, L), v("cp", 0, L)], [v("cp", 0, L)], 4.0, True)
+    for k, (a, b) in enumerate(CH):
+        o = P((3, 5, 6)[k], 0, b - a)
+        pe([(o, IDN, v("crb", a, b), True, False), (o, IDN, v("dd", a, b), False, True)])
+        act(v("rr", a, b), o, F.Sign, -1.0, -2.0 ** -40)
+    fill(v("ycw", OARR, OB), 256.0)
+    fill(v("yaw", OARR, OB), 0.0)
+    zw, hz = W(96), W(96)
+    fill(sub(zw, 80, 96), 0.0)
+    fill(sub(hz, 80, 96), 0.0)
+
+    hu, xlu, xru, pu, iu, kcu, lu, apu = U(), U(), U(), U(160), U(160), U(6), U(6), U(12)
+    on, tw, sh, sx = None, own, None, None
+    tmp = {}
+
+    def t_(name, n=80, buf="w"):
+        if name not in tmp:
+            tmp[name] = new(buf, n)
+        return tmp[name]
+
+    cp(hu, h)
+    for n in (1, 2, 3):
+        slot, nxt, w0, w1 = ((OA_, OB, OU, OB), (OB, OA_, OL, NY), (OA_, OB, OA_, OB))[n - 1]
+        L0, R0, D0, kap_, stamp, lam = OL - w0, OR - w0, DEAD - w0, slot - OL, 2048.0 * n, (0.5, 2.0, 1.0)[n - 1]
+        cA, cB = L0 - stamp - D0, R0 - stamp - D0
+
+        for a, b in ((0, 640), (640, L)):
+            o, x = v("gx", a, b), ind(v("tab", 0, H), lst(hu, a, b))
+            if a and n in OPT["GV"]:
+                op("v", lambda o=o, x=x: g.vector.tensor_copy(ap(o), ap(x)), [x] + tabr, [o], vcost(o, [x]))
+            else:
+                act(o, x, F.Copy, extra=tabr)
+        d64 = n == 1 or n in OPT["DV"]
+        y = conv(P(4, 0, 80), B32 if d64 else B0, v("dd", 0, L))
+        ny = lin(t_("ny"), y, -1.0, 16.0 if d64 else 0.0)
+        if n == 1:
+            on = ts(t_("on1"), ny, -16.0, A.is_gt)
+        a3 = lin(t_("a3"), tt(t_("go"), ts(Q(0), h, float(H0), A.is_lt), on, A.mult), -116.0, 100.0)
+        pxl = conv(P(5, 0, 80), Bxl, v("gx", 0, L))
+        cp(xlu, pxl)
+        xl = act(t_("xl"), pxl, F.Copy)
+        pxr = conv(P(6, 0, 80), Bxr, v("gx", 0, L))
+        cp(xru, pxr)
+        df = tt(t_("df"), pxr, xl, A.subtract)
+        xr = act(t_("xr"), pxr, F.Copy)
+        fn_ = t_("fn", 160, "wb")
+        free, nm = sub(fn_, 0, 80), sub(fn_, 80, 160)
+        lin(free, on, -1.0, 1.0)
+        onq = lin(t_("onq"), on, -1e6, 1e6)
+        sf = scan(t_("sf", 80, "wb"), free)
+        f = P(4, 80, 160)
+        pe([(f, ONES, sf, True, False), (f, NUT, free, False, True), (P(4, 160, 161), ONES, sub(sf, 79, 80), True, True)])
+        p0 = t_("p0", 160)
+        tt(Q(1), f, ownm, A.subtract)
+        ts(Q(2), f, 736.0, A.min, float(XP), A.add)
+        nf = ts(t_("nf", 1), P(4, 160, 161), -2048.0, A.add)
+        tt(sub(p0, 0, 80), tt(Q(1), Q(1), free, A.mult), own, A.add)
+        tt(sub(p0, 80, 160), tt(Q(2), tt(Q(2), Q(2), tw, A.subtract), free, A.mult), tw, A.add)
+        lin(sub(kk, 80, 160), tw, -1.0, float(XF + 2048))
+        owns = lin(t_("owns"), own, 1.0, stamp)
+        rb = col([(6, n)], vb[d64])
+        for k, (a, b) in enumerate(CH):
+            o = P(k, 0, b - a)
+            pe([(o, M64 if d64 else Mdd, v("dd", a, b), True, False)])
+            pe([(o, Mrr, v("rr", a, b), False, False)])
+            pe([(o, MG, v("gx", a, b), False, True)])
+            act(v("pb", a, b), o, F.Relu, 1.0, rb)
+        mrep = None
+        if n > 1:
+            lhn, got = "lh%d" % (n - 1), ("rh%d" % (n - 1), names["rh%d" % (n - 1)])
+            hs = P(3, 0, 192)
+            pe([(sub(hs, 0, 96), ONES, v(lhn, 0, 96), True, True), (sub(hs, 96, 192), SHO, v(lhn, 96, 192), True, True)],
+               xw=got, after=sh)
+            va = ts(Q(4, 192), hs, 0.0, A.is_gt)
+            ap0 = lin(t_("ap0", 192, "wb"), hs, mlo, col([(5, 1), (6, n)], nmlo))
+            sa = scan(t_("sa", 192), va)
+            mrep = act(t_("mrep", 80, "wb"), v("ones", 0, 80), F.Copy, sub(sa, 191, 192))
+            pv = conv(P(3, 192, 204), Bsix, tt(t_("vr", 192, "wb"), va, sa, A.mult))
+            aa = tt(Q(4, 12), tt(Q(4, 12), pv, cs1, A.add), ts(t_("ab_", 12), pv, 0.0, A.is_gt), A.mult)
+            cp(apu, tt(Q(4, 12), aa, cs2, A.add))
+            a0 = L + 192 * (n - 2)
+            tt(ind(v("xw", 0, NX), apu), ap0, v("idc", a0, a0 + 192), A.add)
+        x = conv(P(5, 0, 80), B0, v("rr", 0, L))
+        dis2 = t_("dis", 160, "wb")
+        dis = sub(dis2, 0, 80)
+        nlp, nrp = tt(Q(0), x, ny, A.is_lt), tt(t_("nrp"), x, a3, A.is_gt)
+        tt(dis, nlp, nrp, A.mult)
+        sd = scan(t_("sd", 80, "wb"), dis)
+        items = []
+        for a in (0, 80):
+            o = P(6, a, a + 80)
+            items += [(o, ONES, sd, True, False), (o, NUT, dis, False, False), (o, I2048n, dis, False, mrep is None)]
+            if mrep is not None:
+                items.append((o, O16, mrep, False, True))
+        pe(items)
+        d = P(6, 0, 160)
+        match2 = ts(t_("match", 160), d, nf, A.is_lt)
+        e = tt(Q(2, 160), d, kk, A.add)
+        match = sub(match2, 0, 80)
+        cp(pu, tt(e, tt(e, e, match2, A.mult), p0, A.add))
+        tt(ind(v("xw", 0, NX), sub(pu, 0, 80)), v("pb", 0, L), v("idc", 0, L), A.add)
+        XS = OPT["XS"][n - 1]
+        act(v("xg", 0, XS), ind(v("xw", 0, NX), sub(pu, 80, 80 + XS // 16)), F.Copy)
+        if XS < L:
+            cp(v("xg", XS, L), ind(v("xw", 0, NX), sub(pu, 80 + XS // 16, 160)))
+        for a, b in CH:
+            tt(v("ycw", slot + a, slot + b), ind(v("kt", 0, 3328), lst(hu, a, b)), v("cp", a, b), A.mult)
+        for a, b in ((0, 640), (640, L)):
+            act(v("dl", a, b), ind(v("dt", 0, H), lst(xlu, a, b)), F.Copy)
+            act(v("dr", a, b), ind(v("dt", 0, H), lst(xru, a, b)), F.Copy)
+        bank, mk = 0, 32.0 if n == 1 else 128.0
+        for k, (off, s1, s2) in enumerate(((OL, mk, mk - lam), (OR, -mk, mk + lam), (OU, lam, 0.0))[:3 if n == 1 else 2]):
+            o, part, t = v("vl", k * L, k * L + L), v("ycw", off, off + L), v("ycw", slot, slot + L)
+            if (n, k) in OPT["PV"]:
+                Im, cm = scaled(IDN, s1), scaled(IDN, s2)
+                for j, (a, b) in enumerate(CH):
+                    o = P((3, 0, 1)[j], 0, b - a)
+                    pe([(o, Im, v("rr", a, b), True, False), (o, cm, v("ones", 0, b - a), False, True)])
+                    tt(sub(part, a, b), sub(t, a, b), o, A.add)
+                continue
+            if (n, k) in OPT["VS"]:
+                lin(part, v("rr", 0, L), s1, s2)
+            else:
+                ts(o, v("rr", 0, L), s1, A.mult, s2, A.add)
+                dma("g", ap(part), ap(o), [o], [part], 3.2)
+            dma("g", ap(part), ap(t), [t, part], [part], 4.5, True)
+        for a, b in CH:
+            for src, Im, off in (("dl", I64n, OL), ("dr", I64p, OR)):
+                o = P(bank % 4, 0, b - a)
+                bank += 1
+                pe([(o, IDN, v(src, a, b), True, False), (o, Im, v("rr", a, b), False, True)])
+                act(o, o, F.Sigmoid, 1.0, -64.0)
+                if n == 1 and bank == 1:
+                    ops[-1]["cost"] += 1.3
+                    ops[-1]["hold"] += 1.3
+                tt(v("yaw", off + a, off + b), v("yaw", slot + a, slot + b), o, A.mult)
+        if n == 1:
+            dsum(v("yaw", OU, OU + L), v("yaw", OL, OL + L), v("yaw", OR, OR + L))
+        else:
+            ldn, got, r0 = "ld%d" % (n - 1), ("rd%d" % (n - 1), names["rd%d" % (n - 1)]), OARR + 192 * (n - 2)
+            po = P(0, 0, 192)
+            pe([(po, SHF, v(ldn, 192, 384), True, True)], 4, xw=got, after=sx)
+            for k, buf in enumerate(("ycw", "yaw")):
+                act(v(buf, r0, r0 + 96), v(ldn, 96 * k, 96 * k + 96), F.Copy, xw=got, after=sx)
+                act(v(buf, r0 + 96, r0 + 192), sub(po, 96 * k, 96 * k + 96), F.Copy)
+        wo = conv(P(4, 0, 80), Bw[kap_], v("pb", 0, L))
+        hh, pre = t_("hh", 160), t_("pre", 160)
+        ts(Q(0), wo, 0.0, A.not_equal)
+        tt(Q(1), wo, co1, A.add)
+        tt(Q(2), co2, wo, A.subtract)
+        ld = tt(Q(0), Q(0), df, A.mult)
+        tt(sub(pre, 0, 80), Q(1), on, A.mult)
+        tt(sub(pre, 80, 160), Q(2), match, A.mult)
+        tt(sub(hh, 0, 80), tt(Q(1), xr, ld, A.subtract), on, A.mult)
+        tt(sub(hh, 80, 160), tt(Q(2), xl, ld, A.add), match, A.mult)
+        lin(nm, match, -1.0, 1.0)
+        pw = conv(P(5, 0, 80), Bw[kap_], v("xg", 0, L))
+        pdf = conv(P(6, 0, 80), Bdf, v("xg", 0, L))
+        pl = conv(P(4, 0, 80), Bxl, v("xg", 0, L))
+        plw = ts(t_("plw"), pw, 0.0, A.not_equal)
+        wsa, wsb = lin(t_("wsa"), pw, 1.0, -float(cA)), lin(t_("wsb"), pw, 1.0, float(cB))
+        u1 = conv(P(5, 0, 80), Bid, v("xg", 0, L))
+        e1 = tt(t_("e1"), pdf, plw, A.mult)
+        e2 = tt(t_("e2"), pdf, e1, A.subtract)
+        tt(Q(0), pl, e1, A.add)
+        tt(Q(1), pl, e2, A.add)
+        hp2 = tt(t_("hp2_%d" % (n % 2), 160), tt(Q(0, 160), Q(0, 160), fn_, A.mult), hh, A.add)
+        h = sub(hp2, 0, 80)
+        js = ts(Q(0), h, -3.5, A.add, 100663296.0, A.add)
+        jp = ts(t_("jp"), sub(hp2, 80, 160), -3.5, A.add, 100663296.0, A.add)
+        eq = tt(Q(0), js, jp, A.is_equal)
+        tt(Q(2), u1, wsa, A.subtract)
+        tt(Q(3), u1, wsb, A.add)
+        idd = tt(t_("idd"), u1, owns, A.subtract)
+        q = tt(t_("q"), ts(Q(1), u1, stamp, A.is_lt, 1e6, A.mult), onq, A.min)
+        pvd = ts(Q(1), act(t_("uabs"), u1, F.Abs, 1.0, -(stamp + 639.5)), 640.0, A.is_lt)
+        tw1 = tt(t_("tw1"), pvd, idd, A.mult)
+        ab = tt(Q(2, 160) if n > 1 else t_("ab", 160), tt(Q(2, 160), Q(2, 160), fn_, A.mult), pre, A.add)
+        if n == 1:
+            ts(Q(3), tt(Q(3), sub(ab, 80, 160), sub(ab, 0, 80), A.subtract), 0.5, A.mult, OU - (OL + OR) / 2, A.add)
+        m = tt(Q(0), eq, tw1, A.mult)
+        ol = t_("ol", 160)
+        on2 = tt(sub(ol, 0, 80), m, q, A.is_ge)
+        lo = ts(sub(ol, 80, 160), m, 0.0, A.is_gt)
+        i1, i2 = sub(iu, 0, 80), sub(iu, 80, 160)
+        if n == 1:
+            ts(i1, tt(Q(3), tt(Q(3), tt(Q(3), Q(3), lo, A.mult), sub(ab, 0, 80), A.add), on2, A.mult), float(D0), A.add)
+        else:
+            ts(iu, tt(ab, ab, ol, A.mult), float(D0), A.add)
+        if n < 3:
+            lv = tt(t_("lv", 80, "wb"), ts(Q(0), h, float(H0), A.is_ge), on2, A.mult)
+            sl = scan(t_("sl", 80, "wb"), lv)
+            pe([(P(4, 0, 80), ONES, sl, True, True)])
+            pe([(P(6, 0, 80), ONES, sl, True, False), (P(6, 0, 80), NUT, lv, False, True)])
+            sg = t_("sg", 6)
+            for c in range(6):
+                act(t_("junk%d" % c), P(4, 0, 80), F.Sign, 1.0, sub(jb, c, c + 1), accum=sub(sg, c, c + 1))
+            cp(hu, h)
+            par = ts(t_("par", 80, "wi"), cp(t_("hi", 80, "wi"), h), 1, A.bitwise_and)
+            tt(sub(hz, 0, 80), ts(Q(1), par, -2.0, A.mult, 1.0, A.add), lin(t_("hz0"), h, 1.0, float(1 - H0)), A.mult)
+            z0 = ts(Q(0), P(6, 0, 80), 1.0, A.add)
+            tt(sub(zw, 0, 80), z0, lv, A.mult)
+            gone = tt(Q(0), ts(Q(0), z0, 96.0, A.is_le), lv, A.mult)
+            on = tt(t_("on%d" % (n % 2)), on2, gone, A.subtract)
+            ts(kcu, sg, -0.5, A.mult, 40.0, A.add)
+            kc16 = lin(t_("kc16", 6), sg, -8.0, 640.0)
+            hit = tt(t_("hit", 96, "wb"), ind(zw, kcu), j1, A.is_equal)
+            tt(v("sh%d" % n, 0, 96), ind(hz, kcu), hit, A.mult)
+            sh = send("sh%d" % n, "lh%d" % n, 96, "rh%d" % n)
+            pln = conv(P(5, 0, 6), Bpm, hit)
+            ts(lu, tt(Q(1, 6), pln, kc16, A.add), float(L - 1), A.min)
+            tw = tt(t_("tw"), tw1, own, A.add)
+        else:
+            cp(hu, tt(Q(4), ts(Q(4), h, float(H0), A.is_ge, 256.0, A.mult), h, A.add))
+        wc, wa = v("ycw", w0, w1), v("yaw", w0, w1)
+        for k, (a, b) in enumerate(CH):
+            if n == 1:
+                if k in OPT["CV"]:
+                    ts(v("cp", a, b), ind(wc, lst(i1, a, b)), 8.0, A.mult)
+                else:
+                    act(v("cp", a, b), ind(wc, lst(i1, a, b)), F.Copy, 8.0)
+            else:
+                act(v("g2c", a, b), ind(wc, lst(i2, a, b)), F.Copy)
+                tt(v("cp", a, b), ind(wc, lst(i1, a, b)), v("g2c", a, b), A.min)
+            if n < 3:
+                act(v("rr", a, b), v("cp", a, b), F.Sign, -1.0, -2.0 ** -40)
+                if n + 1 in OPT["DV"]:
+                    ts(v("dd", a, b), v("cp", a, b), 32.0, A.is_gt, 64.0, A.mult)
+                else:
+                    act(v("dd", a, b), v("cp", a, b), F.Sign, 1.0, -32.0)
+        for a, b in CH:
+            if n == 1:
+                act(v("yaw", nxt + a, nxt + b), ind(wa, lst(i1, a, b)), F.Copy)
+            else:
+                act(v("g2a", a, b), ind(wa, lst(i2, a, b)), F.Copy)
+                tt(v("yaw", nxt + a, nxt + b), ind(wa, lst(i1, a, b)), v("g2a", a, b), A.add)
+        if n < 3:
+            sd_ = "sd%d" % n
+            act(v(sd_, 0, 96), ind(v("cp", 0, L), lu), F.Copy, 0.5)
+            act(v(sd_, 96, 192), ind(v("yaw", nxt, nxt + L), lu), F.Copy)
+            sx = send(sd_, "ld%d" % n, 192, "rd%d" % n)
+        else:
+            for k, (a, b) in enumerate(CH):
+                o = P(k, 0, b - a)
+                act(o, v("cp", a, b), F.Sigmoid, -8.0, 240.0)
+                tt(v("oc", a, b), v("cp", a, b), o, A.mult)
+                dma("y", T.yc[:, a:b], T.oc[:, a:b], [v("oc", a, b)], [], 2.2)
+                if k in OPT["KP"]:
+                    o = P(3 + k, 0, b - a)
+                    pe([(o, IDN, act(v("dl", a, b), ind(v("kt", 0, 3328), lst(hu, a, b)), F.Copy), True, True)])
+                    tt(v("oa", a, b), o, v("yaw", nxt + a, nxt + b), A.mult)
+                else:
+                    tt(v("oa", a, b), ind(v("kt", 0, 3328), lst(hu, a, b)), v("yaw", nxt + a, nxt + b), A.mult)
+                dma("y", T.ya[:, a:b], T.oa[:, a:b], [v("oa", a, b)], [], 2.2)
+
+    no = len(ops)
+    succ = [[] for _ in range(no)]
+    for i, o in enumerate(ops):
+        o["pre"] = [(j, LAT) for j in o["deps"]] + ([(o["after"], NET)] if o["after"] is not None else [])
+        for j, lat in o["pre"]:
+            succ[j].append((i, lat))
+    prio = [0.0] * no
+    for i in range(no - 1, -1, -1):
+        prio[i] = ops[i]["cost"] + max([lat + prio[j] for j, lat in succ[i]], default=0.0)
+    pred = [o["pre"] for o in ops]
+
+    def place(pr, before, behind, back):
+        left, ready, start = [len(x) for x in before], [0.0] * no, [0.0] * no
+        cand = [i for i in range(no) if left[i] == 0]
+        busy = {e: 0.0 for e in "vspgy"}
+        off = [o["cost"] - o["hold"] if back else 0.0 for o in ops]
+        while cand:
+            i = min(cand, key=lambda i: (max(busy[ops[i]["e"]], ready[i] + off[i]), -pr[i]))
+            e = ops[i]["e"]
+            lim = max(busy[e], ready[i] + off[i]) + OPT["AL"] * ops[i]["hold"]
+            i = max([j for j in cand if ops[j]["e"] == e and ready[j] + off[j] <= lim], key=lambda j: pr[j])
+            cand.remove(i)
+            o = ops[i]
+            t0 = max(busy[e], ready[i] + off[i])
+            busy[e] = t0 + o["hold"]
+            start[i] = t0 - off[i]
+            for j, lat in behind[i]:
+                ready[j] = max(ready[j], start[i] + o["cost"] + lat)
+                left[j] -= 1
+                if left[j] == 0:
+                    cand.append(j)
+        return start, max(start[i] + ops[i]["cost"] for i in range(no))
+
+    key = str(sorted(OPT.items())) + str((CY, GC, SC, LAT, PC, DM, NET, OV))
+    if key not in KEPT:
+        seed, best = OPT["SEED"], None
+        for it in range(OPT["IT"]):
+            start, end = place(prio, pred, succ, False)
+            if best is None or end < best[0]:
+                best = (end, start)
+            rstart = place([start[i] + ops[i]["cost"] for i in range(no)], succ, pred, True)[0]
+            prio = []
+            for i in range(no):
+                seed = (seed * 1103515245 + 12345) % 2147483648
+                prio.append(rstart[i] + ops[i]["cost"] + OPT["NZ"] * seed / 2147483648)
+        KEPT[key] = best[1]
+    for i in range(no):
+        ops[i]["t"] = KEPT[key][i]
+    order = sorted(range(no), key=lambda i: (ops[i]["t"], i))
+
+    queue = {"v": g.vector, "s": g.scalar, "p": g.tensor, "g": g, "y": g.sync}
+    esem = {"v": "sv", "s": "ss", "p": "sp", "g": "sg"}
+    count = {}
+    known = {e: {} for e in queue}
+    for i in order:
+        o = ops[i]
+        e = o["e"]
+        need = {}
+        for j in o["deps"]:
+            p = ops[j]
+            if p["mark"] is None or (e == "p" and p["e"] == "p"):
+                continue
+            s, c = p["mark"]
+            if known[e].get(s, 0) < c and need.get(s, (0, 0))[0] < c:
+                need[s] = (c, j)
+        for s, (c, j) in sorted(need.items(), key=lambda kv: -ops[kv[1][1]]["t"]):
+            if known[e].get(s, 0) < c:
+                queue[e].wait_ge(T.sem[s], c)
+                for s2, c2 in ops[j]["clock"].items():
+                    known[e][s2] = max(known[e].get(s2, 0), c2)
+        if o["xw"] is not None and known[e].get(o["xw"][0], 0) < o["xw"][1]:
+            queue[e].wait_ge(T.sem[o["xw"][0]], o["xw"][1])
+            known[e][o["xw"][0]] = o["xw"][1]
+        ins = o["fn"]()
+        if o["sem"] == "none":
+            o["mark"] = None
+            continue
+        s, inc = (o["sem"], 16) if o["sem"] else (esem[e], 1)
+        count[s] = count.get(s, 0) + inc
+        ins.then_inc(T.sem[s], inc)
+        o["mark"] = (s, count[s])
+        o["clock"] = dict(known[e])
+        o["clock"][s] = count[s]
+    for s, c in list(count.items()) + list(names.items()):
+        if known["g"].get(s, 0) < c:
+            g.wait_ge(T.sem[s], c)

@@ -2,38 +2,51 @@ from concourse.bass import DstId, RemoteDMATransfer
 from concourse.mybir import AluOpType as A, ActivationFunctionType as F
 
 L, H, H0 = 1280, 3072, 2816
-OU, OA_, OL, OR, OARR, DEAD, OB, NY = 0, 1280, 2560, 3840, 5120, 5504, 5520, 6800
-XF, XP, XD, NX = 1280, 2560, 3312, 3520
+PAD = 16
+ARR, OL, OR = PAD + L, 13 * 128, 23 * 128
+NA, NC = ARR + 384, PAD + OR + L
+XD, XF, XP, NX, NZ = 1296, 1680, 2960, 3712, 1024
+BIG = 4096.0
+HS = BIG - 1024 - 3.5
+M8 = 1.5 * 2.0 ** 26
+TS = BIG - XF
 CH = [(0, 448), (448, 864), (864, 1280)]
-NW, NB, NU, NI = 10240, 9216, 768, 1536
+NW, NB, NU, NI = 8192, 8192, 1536, 1280
 
 SCRATCH = {
-    "kt": ("sbuf", [128, 3328], "bfloat16"), "dt": ("sbuf", [128, H], "bfloat16"), "tab": ("sbuf", [128, H], "bfloat16"),
-    "ycw": ("sbuf", [128, NY], "float32"), "yaw": ("sbuf", [128, NY], "float32"),
-    "idc": ("sbuf", [128, 1664], "bfloat16"), "xw": ("sbuf", [128, NX], "bfloat16"), "ones": ("sbuf", [128, 512], "bfloat16"),
+    "kt": ("sbuf", [128, PAD + H], "bfloat16"), "dt": ("sbuf", [128, H + 16], "bfloat16"),
+    "tab": ("sbuf", [128, PAD + 2 * H], "bfloat16"), "cw": ("sbuf", [128, NC], "float32"),
+    "wa": ("sbuf", [128, NA], "float32"), "idc": ("sbuf", [128, 1664], "bfloat16"),
+    "xw": ("sbuf", [128, NX], "bfloat16"), "zz": ("sbuf", [128, NZ], "bfloat16"), "ones": ("sbuf", [128, 192], "bfloat16"),
     "w": ("sbuf", [128, NW], "float32"), "wb": ("sbuf", [128, NB], "bfloat16"),
     "wu": ("sbuf", [128, NU], "uint16"), "wi": ("sbuf", [128, NI], "int32"),
+    "vl": ("sbuf", [128, 2 * L], "bfloat16"),
 }
-for _n in ("crb", "amb", "rr", "dd", "gx", "dl", "dr", "pb", "xg"):
+SCRATCH["aq"] = ("sbuf", [128, L + 192], "float32")
+SCRATCH["amb"] = ("sbuf", [128, ARR], "bfloat16")
+for _n in ("crb", "crc", "rr", "dd", "gx", "xg", "kb", "db"):
     SCRATCH[_n] = ("sbuf", [128, L], "bfloat16")
-for _n in ("cp", "g2c", "g2a", "oc", "oa"):
+for _n in ("cp", "cq0", "cq1", "cr0", "cr1", "ar", "ff", "oc", "oa"):
     SCRATCH[_n] = ("sbuf", [128, L], "float32")
 for _n in ("1", "2"):
     SCRATCH["sh" + _n] = ("sbuf", [128, 96], "bfloat16")
     SCRATCH["lh" + _n] = ("sbuf", [128, 192], "bfloat16")
-    SCRATCH["sd" + _n] = ("sbuf", [128, 192], "float32")
-    SCRATCH["ld" + _n] = ("sbuf", [128, 384], "float32")
+    for _k in "ca":
+        SCRATCH["s" + _k + _n] = ("sbuf", [128, 96], "float32")
+        SCRATCH["l" + _k + _n] = ("sbuf", [128, 192], "float32")
 for _b in range(8):
     SCRATCH["p%d" % _b] = ("psum", [128, 512], "float32")
-SCRATCH["vl"] = ("sbuf", [128, 3 * L], "bfloat16")
-NDMA = 44
-SEMAPHORES = ["sv", "ss", "sp", "sg", "sent", "rh1", "rh2", "rd1", "rd2"] + ["d%d" % _i for _i in range(NDMA)]
+NDMA = 80
+SEMAPHORES = ["sv", "ss", "sp", "sg", "sent", "rh1", "rh2", "rc1", "rc2", "ra1", "ra2"] + ["d%d" % _i for _i in range(NDMA)]
 TWO = [_n for _n in SCRATCH if SCRATCH[_n][2] in ("bfloat16", "uint16")]
-CY = 0.83e-3 * 1.25
-GC, SC, LAT, NET, OV = 1.56, 3.8, 0.1, 3.0, 0.02
-PC, DM = 0.52e-3, 1.0
-OPT = {"XS": (640, 640, 960), "CV": (0,), "DV": (), "GV": (1,), "VS": ((1, 0), (1, 1), (2, 0), (2, 1), (3, 0), (3, 1)),
-       "PV": (), "KP": (0, 1), "AL": 0.05, "IT": 8, "SEED": 764, "NZ": 0.3}
+CY = 0.83e-3 * 1.2
+GC, SC, LAT, NET, OV = 1.56, 3.8, 0.13, 3.5, 0.05
+PC, DM, BW, GH = 0.5e-3, 1.1, 9 / 38e3, 1.0
+OPT = {"XS": (768, 768, 768), "CS": (768, 768, 768), "XC": (0, 640, 1280), "VS": ((1, 0), (1, 1), (2, 0), (2, 1), (3, 0), (3, 1)),
+       "C2": ("syy",) * 3, "A2": ("yyy", "yyy", "sss"), "FM": (2, 3), "TP": (), "PA": ((0, L),) * 3, "HS": 2 ** 30 - 1 - 2 ** 11, "TI": "vvvsss",
+       "AP": (3,), "XI": "yyyyyy", "DV": (), "KG": 2 ** 40 - 1, "TQ": "ysysysysys",
+       "HINT": (("t1", "x1"), ("t2", "x2"), ("t3", "x3"), ("o2", "f1"), ("o3", "f2")), "AL": 0.3, "IT": 300, "SEED": 764, "NZ": 0.1, "KICK": 2, "KW": 10, "MW": 0.1,
+       "CASES": ((0.85, 1.0), (1.15, 1.0)), "LS": 24000, "LT": 0.2, "LC": 0.6, "LM": 0.4, "LW": 20}
 KEPT = {}
 
 
@@ -72,7 +85,7 @@ def rank_program(g, core, T, topo):
     def psum(x):
         return x[0][0] == "p" and x[0][1:].isdigit()
 
-    def op(eng, fn, R, W, cost, hold=None, sem=None, xw=None, after=None):
+    def op(eng, fn, R, W, cost, hold=None, sem=None, xw=None, after=None, bw=0.0):
         rs, ws = [], []
         for x in R:
             if isinstance(x, tuple):
@@ -84,16 +97,22 @@ def rank_program(g, core, T, topo):
             else:
                 ws.append(x)
         me, deps = len(ops), set()
+        scatter = any(x[0] == "ind" for x in W)
         for x, w in [(x, False) for x in rs] + [(x, True) for x in ws]:
-            ps = psum(x)
-            for (j, a, b, w2, e2) in acc.setdefault(x[0], []):
-                if (ps and e2 != eng) or ((w or w2) and a < x[2] and x[1] < b):
+            for (j, a, b, w2) in acc.setdefault(x[0], []):
+                if (w or w2) and a < x[2] and x[1] < b and not (scatter and ops[j]["scatter"]):
                     deps.add(j)
         for x, w in [(x, False) for x in rs] + [(x, True) for x in ws]:
-            acc[x[0]].append((me, x[1], x[2], w, eng))
+            acc[x[0]].append((me, x[1], x[2], w))
         ops.append({"e": eng, "fn": fn, "deps": deps, "cost": cost, "hold": cost if hold is None else hold, "sem": sem,
+                    "banks": sorted({x[0] for x in rs + ws if psum(x) and x[0] != "p7"}), "bw": bw, "scatter": scatter,
                     "xw": xw, "after": after})
         return me
+
+    tags = {}
+
+    def tag(name, n):
+        tags.setdefault(name + str(n), []).append(len(ops) - 1)
 
     def vcost(o, xs, two=False):
         n = cnt(o)
@@ -107,16 +126,16 @@ def rank_program(g, core, T, topo):
             f = 0.5 if o[0] in TWO and xs[0][0] in TWO else 1.0
         return OV + max(64, n * f) * CY
 
-    def tt(o, a, b, f):
-        op("v", lambda: g.vector.tensor_tensor(ap(o), ap(a), ap(b), f), [a, b], [o], vcost(o, [a, b], True))
+    def tt(o, a, b, f, extra=()):
+        op("v", lambda: g.vector.tensor_tensor(ap(o), ap(a), ap(b), f), [a, b] + list(extra), [o], vcost(o, [a, b], True))
         return o
 
-    def ts(o, a, s1, f1, s2=None, f2=None):
+    def ts(o, a, s1, f1, s2=None, f2=None, xw=None, after=None):
         if f2 is None:
             fn = lambda: g.vector.tensor_scalar(ap(o), ap(a), ap(s1), None, f1)
         else:
             fn = lambda: g.vector.tensor_scalar(ap(o), ap(a), ap(s1), ap(s2), f1, f2)
-        op("v", fn, [a, s1, s2], [o], vcost(o, [a]))
+        op("v", fn, [a, s1, s2], [o], vcost(o, [a]), xw=xw, after=after)
         return o
 
     def cp(o, a):
@@ -146,18 +165,22 @@ def rank_program(g, core, T, topo):
     def lin(o, a, scale, bias):
         return act(o, a, F.Identity, scale, bias)
 
-    def pe(items, wide=1, xw=None, after=None):
+    def pe(items, xw=None, after=None):
         def fn():
             last = None
             for (o, l, r, st, sp) in items:
                 last = g.tensor.matmul(ap(o), ap(l), ap(r), st, sp)
             return last
         op("p", fn, [x[1] for x in items] + [x[2] for x in items], [x[0] for x in items],
-           0.05 + sum(max(64, cnt(x[2])) * wide * PC for x in items), xw=xw, after=after)
+           0.05 + sum(max(64, cnt(x[2])) * (1 if x[2][0] in TWO else 4) * PC for x in items), xw=xw, after=after)
 
-    def conv(o, B, src):
-        n = cnt(src)
-        pe([(o, sub(B, 15 - i, 143 - i), sub(src, i, n, 16), i == 0, i == 15) for i in range(16)])
+    def mm(o, terms, convs=(), late=(), xw=None, after=None):
+        items = list(terms)
+        for B, src in convs:
+            items += [(sub(B, 15 - i, 143 - i), sub(src, i, cnt(src), 16)) for i in range(16)]
+        pe([(o, l, r, i == 0, i == len(items) - 1 and not late) for i, (l, r) in enumerate(items)], xw, after)
+        if late:
+            pe([(o, l, r, False, i == len(late) - 1) for i, (l, r) in enumerate(late)])
         return o
 
     def iota(o, pat, base, mul):
@@ -168,20 +191,33 @@ def rank_program(g, core, T, topo):
         op("g", fn, [], [o], 0.13 + 2 * cnt(o) * CY)
         return o
 
+    def select(o, a, pat, f, c, base, mul):
+        op("g", lambda: g.affine_select(ap(o), ap(a), pat, f, c, base, mul), [a], [o], 0.17 + 2 * cnt(o) * CY)
+        return o
+
     nd = [0]
 
-    def dma(eng, out, in_, R, W, cost, add=False):
+    def dma(eng, out, in_, R, W, size, add=False):
         q = {"y": g.sync, "s": g.scalar, "g": g}[eng]
         s = "d%d" % nd[0]
         nd[0] += 1
         kw = {"accum_op": A.add} if add else {}
-        op(eng, lambda: q.dma_start(out, in_, **kw), R, W, cost * DM, hold=0.6 * DM if eng == "g" else 0.1, sem=s)
+        bw = size * (2 if add else 1) * BW
+        op(eng, lambda: q.dma_start(out, in_, **kw), R, W, (2.4 if eng == "g" else 2.0) * DM + bw,
+           hold=GH if eng == "g" else 0.1, sem=s, bw=bw)
 
-    def dsum(o, a, b):
-        dma("y", ap(o), ap(a), [a], [o], 3.2)
-        dma("g", ap(o), ap(b), [b, o], [o], 4.5, True)
+    def move(eng, o, a, add=False):
+        dma(eng, ap(o), ap(a), [a] + ([o] if add else []), [o], cnt(o) * (2 if o[0] in TWO else 4), add)
 
-    def send(src, land, n, sem):
+    def copy(eng, o, a):
+        if eng == "s":
+            act(o, a, F.Copy)
+        elif eng == "v":
+            cp(o, a)
+        else:
+            move(eng, o, a)
+
+    def send(src, land, sem):
         trs = []
         for k, step in enumerate((1, 3)):
             dst = T.cores[(rank + step) % nr]
@@ -190,10 +226,10 @@ def rank_program(g, core, T, topo):
             half = len(eng) // 2
             m = sum(1 << e for e in eng[k * half:(k + 1) * half])
             trs.append(RemoteDMATransfer(dst_ids=[DstId(rid=rid, pnc=pid)], dma_engine_mask=m, remote_sem=T.sem[sem],
-                                         src=T[src][:], dst=T[land][:, k * n:(k + 1) * n]))
+                                         src=T[src][:], dst=T[land][:, k * 96:(k + 1) * 96]))
             names["sent"] = names.get("sent", 0) + half
             names[sem] = names.get(sem, 0) + half
-        return op("g", lambda: g.remote_dma_fused(trs, local_sem=T.sem.sent), [v(src, 0, n)], [], 0.5, sem="none")
+        return op("g", lambda: g.remote_dma_fused(trs, local_sem=T.sem.sent), [v(src, 0, 96)], [], 0.5, sem="none")
 
     W = lambda n=80: new("w", n)
     Bf = lambda n=80: new("wb", n)
@@ -204,31 +240,56 @@ def rank_program(g, core, T, topo):
     lst = lambda x, a, b: sub(x, a // 16, b // 16)
 
     pli, exi = I32(80), I32(352)
-    dma("s", ap(sub(exi, 0, 176)), T.lf[:, 0:H0], [], [sub(exi, 0, 176)], 2.0)
-    dma("y", ap(sub(exi, 176, 352)), T.rt[:, 0:H0], [], [sub(exi, 176, 352)], 2.0)
-    dma("s", ap(pli), T.place[:], [], [pli], 2.0)
-    dma("y", T.amb[:], T.amp[:], [], [v("amb", 0, L)], 2.4)
-    dma("y", T.crb[:], T.cro[:], [], [v("crb", 0, L)], 2.8)
-    dma("y", T.kt[:, 0:H0], T.kap[:, 0:H0], [v("crb", 0, 1)], [v("kt", 0, H0)], 3.2)
-    dma("y", T.dt[:], T.dam[:], [v("crb", 0, 1)], [v("dt", 0, H)], 4.4)
-    dma("y", T.kt[:, H:H + 256], T.kap[:, H0:H], [v("crb", 0, 1)], [v("kt", H, H + 256)], 4.5)
+    dma("s", ap(sub(exi, 0, 176)), T.lf[:, 0:H0], [], [sub(exi, 0, 176)], 704)
+    dma("y", ap(sub(exi, 176, 352)), T.rt[:, 0:H0], [], [sub(exi, 176, 352)], 704)
+    dma("s", ap(pli), T.place[:], [], [pli], 320)
+    dma("y", T.amb[:, PAD:ARR], T.amp[:], [], [v("amb", PAD, ARR)], 2 * L)
+    dma("y", T.crb[:], T.cro[:], [], [v("crb", 0, L)], 2 * L)
+    dma("y", T.crc[:], T.cro[:], [], [v("crc", 0, L)], 2 * L)
+    dma("y", T.kt[:, PAD:PAD + H0], T.kap[:, 0:H0], [], [v("kt", PAD, PAD + H0)], 2 * H0)
+    dma("y", T.dt[:, 0:H], T.dam[:], [], [v("dt", 0, H)], 2 * H)
 
     pi = iota(I32(1), [[0, 1]], 0, 1)
     xrow = iota(W(144), [[1, 144]], -15, 0)
     g16 = iota(W(128), [[16, 8], [0, 16]], 0, 0)
     ownp = iota(W(80), [[16, 80]], 0, 1)
-    dhi = iota(W(256), [[1, 4], [0, 64]], H0 // 64, 0)
-    dlo = iota(W(256), [[0, 4], [1, 64]], 0, 0)
-    ida = iota(Bf(416), [[1, 26], [0, 16]], 0, 0)
-    idb = iota(Bf(416), [[0, 26], [1, 16]], 0, 0)
-    dma("g", T.yaw[:, OA_:OA_ + L], T.amp[:], [idb, v("kt", 0, 1)], [v("yaw", OA_, OA_ + L)], 4.0)
-    fill(v("xw", 0, 704), 0.0)
-    fill(v("tab", 0, 1408), 0.0)
-    dma("s", T.tab[:, 1408:H0], T.tab[:, 0:1408], [v("tab", 0, 1408)], [v("tab", 1408, H0)], 2.4)
-    fill(v("ones", 0, 512), 1.0)
-    fill(v("kt", H0, H), 0.5)
-    for k in range(1, 5):
-        dma("y", T.xw[:, 704 * k:704 * k + 704], T.xw[:, 0:704], [v("xw", 0, 704), v("crb", 0, 1)], [v("xw", 704 * k, 704 * k + 704)], 3.0)
+    zz = fill(v("zz", 0, NZ), 0.0)
+    zf = iota(W(128), [[0, 128]], 0, 0)
+    nk = [0]
+
+    def const(o, c):
+        nk[0] += 1
+        if not OPT["KG"] >> nk[0] & 1:
+            return fill(o, c)
+        if c == int(c):
+            return iota(o, [[0, cnt(o)]], int(c), 0)
+        return select(o, sub(zz, 0, cnt(o)), [[0, cnt(o)]], A.is_gt, c, 0, 0)
+
+    def zero(e, o):
+        if e == "v":
+            fill(o, 0.0)
+        elif e == "g":
+            iota(o, [[0, cnt(o)]], 0, 0)
+        else:
+            copy(e, o, sub(zz, 0, cnt(o)))
+
+    def ident(c, buf="wb"):
+        nk[0] += 1
+        if OPT["KG"] >> nk[0] & 1:
+            return select(new(buf, 128), sub(zz, 0, 128) if buf == "wb" else zf, [[-1, 128]], A.not_equal, c, 0, 1)
+        return ts(new(buf, 128), IDN if buf == "wb" else IDF, c, A.mult)
+
+    for k in range(2):
+        for j, (a, b) in enumerate(((0, NZ), (NZ, 2 * NZ), (2 * NZ, H))):
+            zero(OPT["TI"][3 * k + j], v("tab", PAD + k * H + a, PAD + k * H + b))
+    for k, o in enumerate([v("xw", a, min(NX, a + NZ)) for a in range(0, NX, NZ)] + [v("idc", 0, NZ), v("idc", NZ, 1664)]):
+        zero(OPT["XI"][k], o)
+    const(v("ones", 0, 192), 1.0)
+    const(v("kt", 0, PAD), 0.0)
+    const(v("kt", PAD + H0, PAD + H), 0.5)
+    const(v("dt", H, H + 16), 20.0)
+    const(v("amb", 0, PAD), 0.0)
+    c8, c35 = const(Bf(), 8.0 / BIG), const(Bf(), -3.5)
     pf = cp(W(1), pi)
     pm = cp(W(1), ts(I32(1), pi, 15, A.bitwise_and))
     t16 = ts(I32(1), pi, 16, A.bitwise_and)
@@ -242,6 +303,7 @@ def rank_program(g, core, T, topo):
     own = ts(W(), ownp, pg, A.subtract)
     ONES = ts(Bf(128), g16, pg, A.is_equal)
     IDN = ts(Bf(128), mrow, pf, A.is_equal)
+    IDF = ts(W(128), mrow, pf, A.is_equal)
     NUT = tt(Bf(128), ts(Q(0, 128), mrow, pf, A.is_le, -1.0, A.mult), ONES, A.mult)
 
     def col(terms, c=None):
@@ -249,76 +311,90 @@ def rank_program(g, core, T, topo):
             c = act(W(1), OH(j), F.Identity, float(wgt), c)
         return c
 
-    def scaled(src, c):
-        return act(Bf(cnt(src)), src, F.Copy, c)
+    def scaled(src, c, buf="wb"):
+        return act(new(buf, cnt(src)), src, F.Copy, c)
 
-    wxl, wxr = col([(0, 64), (4, 1)]), col([(8, 64), (12, 1)])
-    Bxl, Bxr, Bdf = scaled(B0, wxl), scaled(B0, wxr), scaled(B0, lin(W(1), wxl, -1.0, wxr))
-    Bid = scaled(B0, col([(2, 16), (3, 1), (6, 2048)]))
-    wv = col([(5, -1280), (7, 1280)])
-    Bw = {k: scaled(B0, col([(1, k)], wv)) for k in (OA_ - OL, OB - OL)}
-    Bsix, Bpm = scaled(B0, 0.0625), scaled(B0, pm)
-    O16 = scaled(ONES, 0.0625)
-    M57 = tt(Bf(128), sub(B0, 10, 138), sub(B0, 8, 136), A.add)
-    Mrr, Mdd = scaled(M57, -1.0), scaled(M57, -0.5)
-    MG = tt(Bf(128), ts(Q(2, 128), M57, OH(1), A.mult, 64.0, A.mult), IDN, A.add)
-    I2048n, I64p, I64n = [scaled(IDN, c) for c in (-2048.0, 64.0, -64.0)]
-    vb = {True: OH(5), False: col([(5, -7), (7, -8)])}
-    B32, M64 = scaled(B0, 1.0 / 32), scaled(M57, -1.0 / 64)
-    mhi, mlo = col([(0, 1), (8, 1)]), col([(4, 1), (12, 1)])
-    nmlo = act(W(1), mlo, F.Copy, -1.0)
+    nh = [0]
+
+    def half(src, c):
+        nh[0] += 1
+        return scaled(src, c) if OPT["HS"] >> nh[0] & 1 else ts(Bf(cnt(src)), src, c, A.mult)
+
+    wid = col([(2, 104)], OH(3))
+    w0, w8 = col([(0, 8)]), col([(8, 8)])
+    Bhw, Boj, Boc = [half(B0, c) for c in (col([(0, 8)], OH(4)), w8, col([(1, 128)]))]
+    Bc, Bt, Bh = [half(B0, c) for c in (col([(5, OL + OR), (1, -128)], wid), wid, col([(8, 8)], OH(12)))]
+    Bjp = half(B0, col([(5, BIG)], w0))
+    cm8 = const(Bf(), M8 / BIG)
+    B32, B128, Bpm = half(B0, 1 / 32), half(B0, BIG / 32), half(B0, pm)
+    Bd = {1: half(B0, -2.0 ** -23), 2: half(B0, -0.5)}
+    O32 = half(ONES, 1 / 32)
+    Ip, In, I15, Il, Ir, I256, I20 = [ident(c) for c in (BIG, -BIG, H / 2, -OL / 2, (OL - OR) / 2, 256.0, 2.0 ** 20)]
+    F128, FN = ident(-128.0, "w"), ident(-1.0, "w")
+    Iw = {n: ident(2.0 ** (-n - 1)) for n in OPT["FM"]}
     jb = lin(W(6), sub(own, 0, 6), -1.0, -0.5)
-    ownm = lin(W(), own, 1.0, -float(XF))
-    co1, co2 = lin(W(), own, 1.0, float(OR - DEAD)), lin(W(), own, 1.0, float(OL - DEAD))
+    owns = lin(W(), own, 1.0, PAD + TS)
+    ownf, cmpw = W(160), W(160)
+    lin(sub(ownf, 0, 80), own, 1.0, XF - XP + BIG)
+    lin(sub(ownf, 80, 160), own, 1.0, XP - XF + BIG)
+    lin(sub(cmpw, 0, 80), own, 1.0, PAD - XP + BIG)
+    tws = const(sub(cmpw, 80, 160), TS)
     pgn0 = lin(W(1), pg, 1.0, 16.0)
     pgn = tt(W(1), pgn0, ts(W(1), pgn0, 128.0, A.is_ge, 128.0, A.mult), A.subtract)
     SHO = ts(Bf(128), g16, pgn, A.is_equal, -1.0, A.mult)
     SHF = ts(W(128), mrow, lin(W(1), pgn, 1.0, pm), A.is_equal)
-    cs1 = lin(W(12), sub(own, 0, 12), -1.0, float(XP - 1 - XD))
-    cs2 = lin(W(12), sub(own, 0, 12), 1.0, float(XD))
-    kk = W(160)
-    lin(sub(kk, 0, 80), own, -1.0, float(XP + 2048))
+    cs = lin(W(12), sub(own, 0, 12), 1.0, XD - XP + 1 + BIG / 2)
+    jh = lin(W(12), sub(own, 0, 12), 0.5, 0.5)
+    abase = col([(8, -128), (5, -1)])
+    asc = [col([(12, 2)]), col([(12, -2)])]
+    abi = [col([(12, -1)], abase), col([(12, 256)], abase)]
 
-    for k in range(4):
-        a, b = 416 * k, 416 * k + 416
-        if k == 0:
-            pe([(P(0, 0, 416), sub(Bsix, 13, 141), ida, True, False), (P(0, 0, 416), sub(Bsix, 12, 140), idb, False, True)])
-            act(v("idc", a, b), P(0, 0, 416), F.Copy)
-        else:
-            ts(v("idc", a, b), v("idc", 0, 416), col([(2, 26 * k)]), A.add)
+    idr = []
+    for row, src in ((2, act(Bf(104), v("ones", 0, 104), F.Copy, pm)), (3, iota(Bf(104), [[1, 104]], PAD, 0)), (5, v("ones", 0, 104))):
+        idr.append(v("idrow%d" % row, 0, 1))
+        dma("y", T.idc[row:128:16, :], ap(src), [src, v("idc", 0, 1664)], [idr[-1]], 500)
 
     hl, hlb = I32(704), Bf(704)
-    cp(sub(hlb, 0, 352), ts(sub(hl, 0, 352), exi, 6, A.arith_shift_right))
-    cp(sub(hlb, 352, 704), ts(sub(hl, 352, 704), exi, 63, A.bitwise_and))
-    for row, a, e in ((0, 0, "y"), (8, 176, "s"), (4, 352, "y"), (12, 528, "s")):
-        dma(e, T.tab[row:128:16, 0:H0], ap(sub(hlb, a, a + 176)), [sub(hlb, a, a + 176), v("tab", 0, H0)],
-            [v("tabrow%d" % row, 0, 1)], 2.5)
-    tt(v("tab", H0, H), lin(P(4, 0, 256), dhi, mhi, OH(1)), act(W(256), dlo, F.Copy, mlo), A.add)
-    tabr = [v("tabrow%d" % r, 0, 1) for r in (0, 4, 8, 12)]
+    ts(sub(hlb, 0, 352), ts(sub(hl, 0, 352), exi, 3, A.arith_shift_right), -128.0, A.add)
+    cp(sub(hlb, 352, 704), ts(sub(hl, 352, 704), exi, 7, A.bitwise_and))
+    codes = [const(Bf(176), float(c // 128)) for c in (OL, OR)]
+    doors = [lin(Bf(16), iota(W(16), [[1, 2], [0, 8]], H0 // 8 - 128, 0), 1.0, lin(W(1), pm, 2.0, 0.0)),
+             iota(Bf(16), [[0, 2], [1, 8]], 0, 0)]
+    tabr = []
+    for k in range(2):
+        t0 = PAD + k * H
+        rows = [(0, 176 * k), (8, 176 - 176 * k), (4, 352 + 176 * k), (12, 528 - 176 * k)]
+        for j, (row, src) in enumerate([(r, sub(hlb, a, a + 176)) for r, a in rows] + [(1, codes[k])]):
+            tabr.append(v("tabrow%d_%d" % (k, row), 0, 1))
+            dma(OPT["TQ"][5 * k + j], T.tab[row:128:16, t0:t0 + H0], ap(src), [src, v("tab", t0, t0 + H0)], [tabr[-1]], 800)
+        for row, src in zip((0, 4), doors):
+            tabr.append(v("tabdoor%d_%d" % (k, row), 0, 1))
+            dma("y", T.tab[row:128:16, t0 + H0:t0 + H], ap(src), [src, v("tab", t0 + H0, t0 + H)], [tabr[-1]], 200)
+    act(v("tab", 0, PAD), v("ones", 0, PAD), F.Copy, col([(0, -129), (1, -16)]))
 
-    plf, pin, pout, h = cp(W(), pli), W(160), W(160), W()
+    plf, pin, pout, hs = ts(W(), pli, HS, A.add), W(160), W(160), W()
     for u in range(5):
         ts(sub(pin, 32 * u, 32 * u + 16), sub(plf, 16 * u, 16 * u + 16), me_, A.mult)
         act(sub(pin, 32 * u + 16, 32 * u + 32), sub(plf, 16 * u, 16 * u + 16), F.Copy, mo_)
     op("v", lambda: g.vector.transpose(ap(pout), ap(pin)), [pin], [pout], 0.19)
     for u in range(5):
-        tt(sub(h, u, 80, 5), sub(pout, 32 * u, 32 * u + 16), sub(pout, 32 * u + 16, 32 * u + 32), A.add)
+        tt(sub(hs, u, 80, 5), sub(pout, 32 * u, 32 * u + 16), sub(pout, 32 * u + 16, 32 * u + 32), A.add)
 
-    ts(v("dd", 0, L), v("amb", 0, L), 0.0, A.is_equal, 64.0, A.mult)
-    dma("g", T.cp[:], T.cro[:], [dlo], [v("cp", 0, L)], 4.0)
-    dma("g", T.cp[:], T.dd[:], [v("dd", 0, L), v("cp", 0, L)], [v("cp", 0, L)], 4.0, True)
+    ts(v("dd", 0, L), v("amb", PAD, ARR), 0.0, A.is_equal, 2.0 ** 23, A.mult)
+    move("g", v("crc", 0, L), v("dd", 0, L), True)
     for k, (a, b) in enumerate(CH):
-        o = P((3, 5, 6)[k], 0, b - a)
-        pe([(o, IDN, v("crb", a, b), True, False), (o, IDN, v("dd", a, b), False, True)])
+        o = mm(P(5 + k % 2, 0, b - a), [(IDN, v("crb", a, b)), (IDN, v("dd", a, b))])
         act(v("rr", a, b), o, F.Sign, -1.0, -2.0 ** -40)
-    fill(v("ycw", OARR, OB), 256.0)
-    fill(v("yaw", OARR, OB), 0.0)
+    for buf in ("cw", "wa"):
+        const(v(buf, 0, PAD), 0.0)
+        for a in range(ARR, NA, 128):
+            move("y", v(buf, a, a + 128), zf)
     zw, hz = W(96), W(96)
-    fill(sub(zw, 80, 96), 0.0)
-    fill(sub(hz, 80, 96), 0.0)
+    const(sub(zw, 80, 96), 0.0)
+    const(sub(hz, 80, 96), 0.0)
 
-    hu, xlu, xru, pu, iu, kcu, lu, apu = U(), U(), U(), U(160), U(160), U(6), U(6), U(12)
-    on, tw, sh, sx = None, own, None, None
+    hu, giu, puw, pur, ic, kcu, apu = U(), U(), U(), U(), U(), U(6), U(12)
+    non, stay, sent = None, None, {}
     tmp = {}
 
     def t_(name, n=80, buf="w"):
@@ -326,290 +402,367 @@ def rank_program(g, core, T, topo):
             tmp[name] = new(buf, n)
         return tmp[name]
 
-    cp(hu, h)
+    rr, dd, gx, xg, xwin = v("rr", 0, L), v("dd", 0, L), v("gx", 0, L), v("xg", 0, L), v("xw", 0, NX)
+    ts(hu, hs, PAD - HS, A.add)
     for n in (1, 2, 3):
-        slot, nxt, w0, w1 = ((OA_, OB, OU, OB), (OB, OA_, OL, NY), (OA_, OB, OA_, OB))[n - 1]
-        L0, R0, D0, kap_, stamp, lam = OL - w0, OR - w0, DEAD - w0, slot - OL, 2048.0 * n, (0.5, 2.0, 1.0)[n - 1]
-        cA, cB = L0 - stamp - D0, R0 - stamp - D0
-
-        for a, b in ((0, 640), (640, L)):
-            o, x = v("gx", a, b), ind(v("tab", 0, H), lst(hu, a, b))
-            if a and n in OPT["GV"]:
-                op("v", lambda o=o, x=x: g.vector.tensor_copy(ap(o), ap(x)), [x] + tabr, [o], vcost(o, [x]))
-            else:
-                act(o, x, F.Copy, extra=tabr)
-        d64 = n == 1 or n in OPT["DV"]
-        y = conv(P(4, 0, 80), B32 if d64 else B0, v("dd", 0, L))
-        ny = lin(t_("ny"), y, -1.0, 16.0 if d64 else 0.0)
+        lam, mk = ((0.5, 2.0 ** 22), (2.0 ** -19, 16.0), (2.0 ** -20, 8.0))[n - 1]
+        ia, i2, fi, lu = U(), U(), U(), U(6)
         if n == 1:
-            on = ts(t_("on1"), ny, -16.0, A.is_gt)
-        a3 = lin(t_("a3"), tt(t_("go"), ts(Q(0), h, float(H0), A.is_lt), on, A.mult), -116.0, 100.0)
-        pxl = conv(P(5, 0, 80), Bxl, v("gx", 0, L))
-        cp(xlu, pxl)
-        xl = act(t_("xl"), pxl, F.Copy)
-        pxr = conv(P(6, 0, 80), Bxr, v("gx", 0, L))
-        cp(xru, pxr)
-        df = tt(t_("df"), pxr, xl, A.subtract)
-        xr = act(t_("xr"), pxr, F.Copy)
-        fn_ = t_("fn", 160, "wb")
-        free, nm = sub(fn_, 0, 80), sub(fn_, 80, 160)
-        lin(free, on, -1.0, 1.0)
-        onq = lin(t_("onq"), on, -1e6, 1e6)
-        sf = scan(t_("sf", 80, "wb"), free)
-        f = P(4, 80, 160)
-        pe([(f, ONES, sf, True, False), (f, NUT, free, False, True), (P(4, 160, 161), ONES, sub(sf, 79, 80), True, True)])
-        p0 = t_("p0", 160)
-        tt(Q(1), f, ownm, A.subtract)
-        ts(Q(2), f, 736.0, A.min, float(XP), A.add)
-        nf = ts(t_("nf", 1), P(4, 160, 161), -2048.0, A.add)
-        tt(sub(p0, 0, 80), tt(Q(1), Q(1), free, A.mult), own, A.add)
-        tt(sub(p0, 80, 160), tt(Q(2), tt(Q(2), Q(2), tw, A.subtract), free, A.mult), tw, A.add)
-        lin(sub(kk, 80, 160), tw, -1.0, float(XF + 2048))
-        owns = lin(t_("owns"), own, 1.0, stamp)
-        rb = col([(6, n)], vb[d64])
-        for k, (a, b) in enumerate(CH):
-            o = P(k, 0, b - a)
-            pe([(o, M64 if d64 else Mdd, v("dd", a, b), True, False)])
-            pe([(o, Mrr, v("rr", a, b), False, False)])
-            pe([(o, MG, v("gx", a, b), False, True)])
-            act(v("pb", a, b), o, F.Relu, 1.0, rb)
-        mrep = None
+            stay, vb = [(Ip, ts(Bf(), hs, H0 + HS, A.is_ge))], 16.0
+        else:
+            vb = 16.0 + BIG
+        np_ = mm(P(1, 0, 80), [(Ip, c8)] * (2 if n == 1 or n in OPT["DV"] else 1), [(Bd[min(n, 2)], dd)])
+        nb = act(t_("nb", 80, "wb"), np_, F.Copy, 1 / BIG)
+        vp = mm(P(0, 0, 80), [], [(B0, rr)], stay + [(In, nb)])
+        if n == 1:
+            non = ts(t_("non", 80, "wb"), np_, 0.5, A.is_gt, -1.0, A.mult)
+        av = act(t_("av"), vp, F.Abs, 1.0, vb)
+        sgn = act(t_("sgn", 80, "wb"), vp, F.Sign, 1.0, vb - 0.5)
+        ts(giu, mm(P(4, 0, 80), [(IDF, hs), (In, non), (In, non), (I15, sgn)]), PAD - HS + H / 2 - 2 * BIG, A.add)
+        XC = OPT["XC"]
+        for a, b in zip(XC, XC[1:]):
+            act(v("gx", a, b), ind(v("tab", 0, PAD + 2 * H), lst(giu, a, b)), F.Copy, extra=tabr)
+            tag("g", n)
+        sn = scan(t_("sn", 80, "wb"), non)
+        fp = P(2, 0, 160)
+        for a in (0, 80):
+            mm(sub(fp, a, a + 80), [(IDF, sub(ownf, a, a + 80)), (ONES, sn), (NUT, non), (Ip, non), (Ip, non)])
+        nfb = lin(t_("nfb", 1), mm(P(2, 160, 161), [(ONES, sub(sn, 79, 80))]), -1.0, BIG - L + 0.5)
+        p0 = tt(t_("p0", 160), fp, cmpw, A.max)
+        more = []
         if n > 1:
             lhn, got = "lh%d" % (n - 1), ("rh%d" % (n - 1), names["rh%d" % (n - 1)])
-            hs = P(3, 0, 192)
-            pe([(sub(hs, 0, 96), ONES, v(lhn, 0, 96), True, True), (sub(hs, 96, 192), SHO, v(lhn, 96, 192), True, True)],
-               xw=got, after=sh)
-            va = ts(Q(4, 192), hs, 0.0, A.is_gt)
-            ap0 = lin(t_("ap0", 192, "wb"), hs, mlo, col([(5, 1), (6, n)], nmlo))
-            sa = scan(t_("sa", 192), va)
-            mrep = act(t_("mrep", 80, "wb"), v("ones", 0, 80), F.Copy, sub(sa, 191, 192))
-            pv = conv(P(3, 192, 204), Bsix, tt(t_("vr", 192, "wb"), va, sa, A.mult))
-            aa = tt(Q(4, 12), tt(Q(4, 12), pv, cs1, A.add), ts(t_("ab_", 12), pv, 0.0, A.is_gt), A.mult)
-            cp(apu, tt(Q(4, 12), aa, cs2, A.add))
+            ha = P(3, 0, 192)
+            pe([(sub(ha, 0, 96), ONES, v(lhn, 0, 96), True, True), (sub(ha, 96, 192), SHO, v(lhn, 96, 192), True, True)],
+               xw=got, after=sent["h"])
+            va = act(t_("va", 192, "wb"), ha, F.Sign, 1.0, -0.25, accum=t_("msum", 1))
+            ap0 = t_("ap0", 192, "wb")
+            for k in range(2):
+                lin(sub(ap0, 96 * k, 96 * k + 96), sub(ha, 96 * k, 96 * k + 96), asc[k], abi[k])
+            sa = scan(t_("sa", 192, "wb"), va)
+            more = [(O32, lin(t_("mrep", 80, "wb"), v("ones", 0, 80), 192.0, t_("msum", 1)))]
+            pv = mm(P(3, 192, 204), [(IDF, jh)], [(B128, va), (B32, sa)])
+            ts(apu, tt(Q(4, 12), pv, cs, A.max), XP - 1 - BIG / 2, A.add)
             a0 = L + 192 * (n - 2)
-            tt(ind(v("xw", 0, NX), apu), ap0, v("idc", a0, a0 + 192), A.add)
-        x = conv(P(5, 0, 80), B0, v("rr", 0, L))
-        dis2 = t_("dis", 160, "wb")
-        dis = sub(dis2, 0, 80)
-        nlp, nrp = tt(Q(0), x, ny, A.is_lt), tt(t_("nrp"), x, a3, A.is_gt)
-        tt(dis, nlp, nrp, A.mult)
+            tt(ind(xwin, apu), ap0, v("idc", a0, a0 + 192), A.add, idr)
+        dis = tt(t_("dis", 80, "wb"), np_, av, A.is_gt)
         sd = scan(t_("sd", 80, "wb"), dis)
-        items = []
-        for a in (0, 80):
-            o = P(6, a, a + 80)
-            items += [(o, ONES, sd, True, False), (o, NUT, dis, False, False), (o, I2048n, dis, False, mrep is None)]
-            if mrep is not None:
-                items.append((o, O16, mrep, False, True))
-        pe(items)
-        d = P(6, 0, 160)
-        match2 = ts(t_("match", 160), d, nf, A.is_lt)
-        e = tt(Q(2, 160), d, kk, A.add)
-        match = sub(match2, 0, 80)
-        cp(pu, tt(e, tt(e, e, match2, A.mult), p0, A.add))
-        tt(ind(v("xw", 0, NX), sub(pu, 0, 80)), v("pb", 0, L), v("idc", 0, L), A.add)
+        rank_d = more + [(NUT, dis), (ONES, sd)]
+        sgm = act(t_("sgm", 80, "wb"), mm(P(3, 208, 288), [(In, dis)] + rank_d), F.Sign, 1.0, nfb)
+        cm = mm(P(1, 320, 400), rank_d + [(In, sgm)])
+        ts(puw, tt(Q(0), cm, sub(p0, 0, 80), A.max), XP - BIG, A.add)
+        for a, b in zip(XC, XC[1:]):
+            tt(ind(xwin, lst(puw, a, b)), v("gx", a, b), v("idc", a, b), A.add, idr)
+            tag("x", n)
+        ts(pur, tt(Q(1), cm, sub(p0, 80, 160), A.max), XF - BIG, A.add, XP + 736.0, A.min)
         XS = OPT["XS"][n - 1]
-        act(v("xg", 0, XS), ind(v("xw", 0, NX), sub(pu, 80, 80 + XS // 16)), F.Copy)
+        act(v("xg", 0, XS), ind(xwin, lst(pur, 0, XS)), F.Copy)
         if XS < L:
-            cp(v("xg", XS, L), ind(v("xw", 0, NX), sub(pu, 80 + XS // 16, 160)))
-        for a, b in CH:
-            tt(v("ycw", slot + a, slot + b), ind(v("kt", 0, 3328), lst(hu, a, b)), v("cp", a, b), A.mult)
-        for a, b in ((0, 640), (640, L)):
-            act(v("dl", a, b), ind(v("dt", 0, H), lst(xlu, a, b)), F.Copy)
-            act(v("dr", a, b), ind(v("dt", 0, H), lst(xru, a, b)), F.Copy)
-        bank, mk = 0, 32.0 if n == 1 else 128.0
-        for k, (off, s1, s2) in enumerate(((OL, mk, mk - lam), (OR, -mk, mk + lam), (OU, lam, 0.0))[:3 if n == 1 else 2]):
-            o, part, t = v("vl", k * L, k * L + L), v("ycw", off, off + L), v("ycw", slot, slot + L)
-            if (n, k) in OPT["PV"]:
-                Im, cm = scaled(IDN, s1), scaled(IDN, s2)
-                for j, (a, b) in enumerate(CH):
-                    o = P((3, 0, 1)[j], 0, b - a)
-                    pe([(o, Im, v("rr", a, b), True, False), (o, cm, v("ones", 0, b - a), False, True)])
-                    tt(sub(part, a, b), sub(t, a, b), o, A.add)
-                continue
-            if (n, k) in OPT["VS"]:
-                lin(part, v("rr", 0, L), s1, s2)
-            else:
-                ts(o, v("rr", 0, L), s1, A.mult, s2, A.add)
-                dma("g", ap(part), ap(o), [o], [part], 3.2)
-            dma("g", ap(part), ap(t), [t, part], [part], 4.5, True)
-        for a, b in CH:
-            for src, Im, off in (("dl", I64n, OL), ("dr", I64p, OR)):
-                o = P(bank % 4, 0, b - a)
-                bank += 1
-                pe([(o, IDN, v(src, a, b), True, False), (o, Im, v("rr", a, b), False, True)])
-                act(o, o, F.Sigmoid, 1.0, -64.0)
-                if n == 1 and bank == 1:
-                    ops[-1]["cost"] += 1.3
-                    ops[-1]["hold"] += 1.3
-                tt(v("yaw", off + a, off + b), v("yaw", slot + a, slot + b), o, A.mult)
-        if n == 1:
-            dsum(v("yaw", OU, OU + L), v("yaw", OL, OL + L), v("yaw", OR, OR + L))
-        else:
-            ldn, got, r0 = "ld%d" % (n - 1), ("rd%d" % (n - 1), names["rd%d" % (n - 1)]), OARR + 192 * (n - 2)
-            po = P(0, 0, 192)
-            pe([(po, SHF, v(ldn, 192, 384), True, True)], 4, xw=got, after=sx)
-            for k, buf in enumerate(("ycw", "yaw")):
-                act(v(buf, r0, r0 + 96), v(ldn, 96 * k, 96 * k + 96), F.Copy, xw=got, after=sx)
-                act(v(buf, r0 + 96, r0 + 192), sub(po, 96 * k, 96 * k + 96), F.Copy)
-        wo = conv(P(4, 0, 80), Bw[kap_], v("pb", 0, L))
-        hh, pre = t_("hh", 160), t_("pre", 160)
-        ts(Q(0), wo, 0.0, A.not_equal)
-        tt(Q(1), wo, co1, A.add)
-        tt(Q(2), co2, wo, A.subtract)
-        ld = tt(Q(0), Q(0), df, A.mult)
-        tt(sub(pre, 0, 80), Q(1), on, A.mult)
-        tt(sub(pre, 80, 160), Q(2), match, A.mult)
-        tt(sub(hh, 0, 80), tt(Q(1), xr, ld, A.subtract), on, A.mult)
-        tt(sub(hh, 80, 160), tt(Q(2), xl, ld, A.add), match, A.mult)
-        lin(nm, match, -1.0, 1.0)
-        pw = conv(P(5, 0, 80), Bw[kap_], v("xg", 0, L))
-        pdf = conv(P(6, 0, 80), Bdf, v("xg", 0, L))
-        pl = conv(P(4, 0, 80), Bxl, v("xg", 0, L))
-        plw = ts(t_("plw"), pw, 0.0, A.not_equal)
-        wsa, wsb = lin(t_("wsa"), pw, 1.0, -float(cA)), lin(t_("wsb"), pw, 1.0, float(cB))
-        u1 = conv(P(5, 0, 80), Bid, v("xg", 0, L))
-        e1 = tt(t_("e1"), pdf, plw, A.mult)
-        e2 = tt(t_("e2"), pdf, e1, A.subtract)
-        tt(Q(0), pl, e1, A.add)
-        tt(Q(1), pl, e2, A.add)
-        hp2 = tt(t_("hp2_%d" % (n % 2), 160), tt(Q(0, 160), Q(0, 160), fn_, A.mult), hh, A.add)
-        h = sub(hp2, 0, 80)
-        js = ts(Q(0), h, -3.5, A.add, 100663296.0, A.add)
-        jp = ts(t_("jp"), sub(hp2, 80, 160), -3.5, A.add, 100663296.0, A.add)
-        eq = tt(Q(0), js, jp, A.is_equal)
-        tt(Q(2), u1, wsa, A.subtract)
-        tt(Q(3), u1, wsb, A.add)
-        idd = tt(t_("idd"), u1, owns, A.subtract)
-        q = tt(t_("q"), ts(Q(1), u1, stamp, A.is_lt, 1e6, A.mult), onq, A.min)
-        pvd = ts(Q(1), act(t_("uabs"), u1, F.Abs, 1.0, -(stamp + 639.5)), 640.0, A.is_lt)
-        tw1 = tt(t_("tw1"), pvd, idd, A.mult)
-        ab = tt(Q(2, 160) if n > 1 else t_("ab", 160), tt(Q(2, 160), Q(2, 160), fn_, A.mult), pre, A.add)
-        if n == 1:
-            ts(Q(3), tt(Q(3), sub(ab, 80, 160), sub(ab, 0, 80), A.subtract), 0.5, A.mult, OU - (OL + OR) / 2, A.add)
-        m = tt(Q(0), eq, tw1, A.mult)
-        ol = t_("ol", 160)
-        on2 = tt(sub(ol, 0, 80), m, q, A.is_ge)
-        lo = ts(sub(ol, 80, 160), m, 0.0, A.is_gt)
-        i1, i2 = sub(iu, 0, 80), sub(iu, 80, 160)
-        if n == 1:
-            ts(i1, tt(Q(3), tt(Q(3), tt(Q(3), Q(3), lo, A.mult), sub(ab, 0, 80), A.add), on2, A.mult), float(D0), A.add)
-        else:
-            ts(iu, tt(ab, ab, ol, A.mult), float(D0), A.add)
+            cp(v("xg", XS, L), ind(xwin, lst(pur, XS, L)))
         if n < 3:
-            lv = tt(t_("lv", 80, "wb"), ts(Q(0), h, float(H0), A.is_ge), on2, A.mult)
+            for a, b in ((0, NZ), (NZ, ARR), (XP, XP + 736)):
+                move("y", v("xw", a, b), sub(zz, 0, b - a))
+        t = v("cw", PAD, ARR)
+        for k, (a, b) in enumerate(CH):
+            kh = ind(v("kt", 0, PAD + H), lst(hu, a, b))
+            if (n, k) in OPT["TP"]:
+                o = mm(P(5 + k % 2, 0, b - a), [(IDN, act(v("kb", a, b), kh, F.Copy))])
+                tt(sub(t, a, b), o, v("cp" if n > 1 else "crc", a, b), A.mult)
+            else:
+                tt(sub(t, a, b), kh, v("cp" if n > 1 else "crc", a, b), A.mult)
+            tag("t", n)
+        if n == 3:
+            dma("y", T.kt[:, PAD + H0:PAD + H], T.kap[:, H0:H], [], [v("kt", PAD + H0, PAD + H)], 512)
+        for k, (off, s1, s2) in enumerate(((OL, mk, mk - lam), (OR, -mk, mk + lam))):
+            o, part = v("vl", k * L, k * L + L), v("cw", PAD + off, ARR + off)
+            if (n, k) in OPT["VS"]:
+                for a, b in CH:
+                    lin(sub(part, a, b), sub(rr, a, b), s1, s2)
+                    tag("o", n)
+                PA = OPT["PA"][n - 1]
+                for a, b in zip(PA, PA[1:]):
+                    move("g", sub(part, a, b), sub(t, a, b), True)
+            else:
+                ts(o, rr, s1, A.mult, s2, A.add)
+                move("y", part, t)
+                move("g", part, o, True)
+        if n > 1:
+            r0 = ARR + 192 * (n - 2)
+            for k, (c, buf) in enumerate((("c", "cw"), ("a", "wa"))):
+                ldn, got = "l%s%d" % (c, n - 1), ("r%s%d" % (c, n - 1), names["r%s%d" % (c, n - 1)])
+                po = mm(P(2, 256 + 96 * k, 352 + 96 * k), [(SHF, v(ldn, 96, 192))], xw=got, after=sent[c])
+                o = v("aq", L, L + 192) if c == "a" and n in OPT["AP"] else v(buf, r0, r0 + 192)
+                act(sub(o, 0, 96), v(ldn, 0, 96), F.Copy, xw=got, after=sent[c])
+                act(sub(o, 96, 192), po, F.Copy)
+        oc = lin(t_("oc"), mm(P(4, 240, 320), [(IDF, owns)], [(Boc, gx)]), 1.0, -TS)
+        ojm = lin(t_("ojm"), mm(P(1, 400, 480), [(In, sgm)], [(Boj, gx)]), 1.0, M8)
+        hw = lin(t_("hw"), mm(P(4, 320, 400), [], [(Bhw, gx)]), 1.0, HS + 1024)
+        icf = tt(t_("icf"), mm(P(0, 80, 160), [(Ip, non), (Ip, non)], [(Bc, xg)]), oc, A.max)
+        cp(ic, icf)
+        hs = tt(t_("hs%d" % (n % 2)), mm(P(4, 80, 160), [(Ip, non), (Ip, v("ones", 0, 80)), (IDN, c35)], [(Bh, xg)]), hw, A.max)
+        js = lin(t_("js"), hs, 1.0, M8)
+        jp = tt(Q(2), mm(P(1, 80, 160), [(Ip, cm8)], [(Bjp, xg)]), ojm, A.max)
+        ne = tt(t_("ne", 80, "wb"), jp, js, A.not_equal)
+        lin(tws, mm(P(3, 288, 368), [], [(Bt, xg)]), 1.0, TS)
+        ts(i2, tt(Q(3), mm(P(0, 240, 320), [(IDF, tws), (In, ne)]), owns, A.max), -(PAD + TS), A.add)
+        none = act(t_("none", 80, "wb"), icf, F.Relu, -2.0, 2.0)
+        on2 = tt(t_("on2", 80, "wb"), mm(P(2, 176, 256), [(IDF, tws), (In, none), (Ip, ne)]), owns, A.is_ge)
+        s1, s2 = [act(t_("s%d" % c, 80, "wb"), icf, F.Sign, 1.0, 0.5 - PAD - c) for c in (OL, OR)]
+        ts(fi, mm(P(4, 160, 240), [(IDF, hs), (In, s1)]), BIG - HS, A.add, float(H), A.min)
+        i2a, drop = i2, []
+        if n in OPT["AP"]:
+            s0 = act(t_("s0", 80, "wb"), icf, F.Sign, 1.0, 0.5 - ARR)
+            ya_ = lin(t_("ya_"), mm(P(0, 320, 400), [(IDF, icf), (Ip, s0), (In, s1)]), 1.0, L - r0 + PAD + TS - 2 * BIG)
+            i2a, drop = ts(U(), tt(Q(5), Q(3), ya_, A.max), -(PAD + TS), A.add), [(In, s0), (Ip, s1)]
+        ts(ia, mm(P(4, 400, 480), [(IDF, icf), (Il, s1), (Ir, s2)] + drop), -OR / 2, A.add)
+        ho = mm(P(0, 160, 240), [(IDF, hs), (Ip, on2)])
+        if n < 3:
+            lv = ts(t_("lv", 80, "wb"), ho, H0 + HS + BIG, A.is_ge)
+            stay = [(In, on2), (Ip, lv)]
             sl = scan(t_("sl", 80, "wb"), lv)
-            pe([(P(4, 0, 80), ONES, sl, True, True)])
-            pe([(P(6, 0, 80), ONES, sl, True, False), (P(6, 0, 80), NUT, lv, False, True)])
+            r1 = mm(P(1, 240, 320), [(ONES, sl)])
+            r2 = mm(P(2, 0, 80), [(In, lv), (Ip, on2), (Ip, on2), (NUT, lv), (ONES, sl)])
             sg = t_("sg", 6)
             for c in range(6):
-                act(t_("junk%d" % c), P(4, 0, 80), F.Sign, 1.0, sub(jb, c, c + 1), accum=sub(sg, c, c + 1))
-            cp(hu, h)
-            par = ts(t_("par", 80, "wi"), cp(t_("hi", 80, "wi"), h), 1, A.bitwise_and)
-            tt(sub(hz, 0, 80), ts(Q(1), par, -2.0, A.mult, 1.0, A.add), lin(t_("hz0"), h, 1.0, float(1 - H0)), A.mult)
-            z0 = ts(Q(0), P(6, 0, 80), 1.0, A.add)
-            tt(sub(zw, 0, 80), z0, lv, A.mult)
-            gone = tt(Q(0), ts(Q(0), z0, 96.0, A.is_le), lv, A.mult)
-            on = tt(t_("on%d" % (n % 2)), on2, gone, A.subtract)
+                act(t_("junk%d" % c), r1, F.Sign, 1.0, sub(jb, c, c + 1), accum=sub(sg, c, c + 1))
+            lin(sub(zw, 0, 80), r2, 1.0, 1.0 - BIG)
+            non = ts(t_("non", 80, "wb"), r2, BIG + 96, A.is_ge, -1.0, A.mult)
+            ts(hu, hs, PAD - HS, A.add)
+            kb = lin(t_("kb", 80, "wb"), hs, 0.499, 128.0 - 0.499 * (H0 + HS))
+            lin(sub(hz, 0, 80), mm(P(3, 368, 448), [(F128, hs), (I256, kb), (IDN, kb)]), 1.0,
+                128.0 * (H0 + HS) - 257 * 128 + 0.5)
             ts(kcu, sg, -0.5, A.mult, 40.0, A.add)
             kc16 = lin(t_("kc16", 6), sg, -8.0, 640.0)
             hit = tt(t_("hit", 96, "wb"), ind(zw, kcu), j1, A.is_equal)
             tt(v("sh%d" % n, 0, 96), ind(hz, kcu), hit, A.mult)
-            sh = send("sh%d" % n, "lh%d" % n, 96, "rh%d" % n)
-            pln = conv(P(5, 0, 6), Bpm, hit)
-            ts(lu, tt(Q(1, 6), pln, kc16, A.add), float(L - 1), A.min)
-            tw = tt(t_("tw"), tw1, own, A.add)
+            sent["h"] = send("sh%d" % n, "lh%d" % n, "rh%d" % n)
+            ts(lu, mm(P(1, 480, 486), [(IDF, kc16)], [(Bpm, hit)]), float(L - 1), A.min)
         else:
-            cp(hu, tt(Q(4), ts(Q(4), h, float(H0), A.is_ge, 256.0, A.mult), h, A.add))
-        wc, wa = v("ycw", w0, w1), v("yaw", w0, w1)
+            ts(hu, ho, PAD - HS - BIG, A.add)
+        CS, sc = OPT["CS"][n - 1], 2.0 ** -17 if n == 1 else 1.0
+        cq = "cq%d" % (n % 2)
+        for a, b in ((0, CS // 32 * 16), (CS // 32 * 16, CS)):
+            act(v(cq, a, b), ind(v("cw", 0, NC), lst(ic, a, b)), F.Copy, sc)
+        if CS < L:
+            ts(v(cq, CS, L), ind(v("cw", 0, NC), lst(ic, CS, L)), sc, A.mult)
+        cr = "cr%d" % (n % 2)
         for k, (a, b) in enumerate(CH):
-            if n == 1:
-                if k in OPT["CV"]:
-                    ts(v("cp", a, b), ind(wc, lst(i1, a, b)), 8.0, A.mult)
-                else:
-                    act(v("cp", a, b), ind(wc, lst(i1, a, b)), F.Copy, 8.0)
-            else:
-                act(v("g2c", a, b), ind(wc, lst(i2, a, b)), F.Copy)
-                tt(v("cp", a, b), ind(wc, lst(i1, a, b)), v("g2c", a, b), A.min)
+            copy(OPT["C2"][n - 1][k], v(cr, a, b), v(cq, a, b))
+            tt(v("cp", a, b), ind(v(cq, 0, L), lst(i2, a, b)), v(cr, a, b), A.min)
+            tag("c", n)
             if n < 3:
-                act(v("rr", a, b), v("cp", a, b), F.Sign, -1.0, -2.0 ** -40)
                 if n + 1 in OPT["DV"]:
-                    ts(v("dd", a, b), v("cp", a, b), 32.0, A.is_gt, 64.0, A.mult)
+                    ts(v("dd", a, b), v("cp", a, b), 1.0, A.is_gt, 2.0, A.mult)
                 else:
-                    act(v("dd", a, b), v("cp", a, b), F.Sign, 1.0, -32.0)
-        for a, b in CH:
-            if n == 1:
-                act(v("yaw", nxt + a, nxt + b), ind(wa, lst(i1, a, b)), F.Copy)
-            else:
-                act(v("g2a", a, b), ind(wa, lst(i2, a, b)), F.Copy)
-                tt(v("yaw", nxt + a, nxt + b), ind(wa, lst(i1, a, b)), v("g2a", a, b), A.add)
+                    act(v("dd", a, b), v("cp", a, b), F.Sign, 1.0, -1.0)
+                act(v("rr", a, b), v("cp", a, b), F.Sign, -1.0, -2.0 ** -60)
+                tag("r", n)
         if n < 3:
-            sd_ = "sd%d" % n
-            act(v(sd_, 0, 96), ind(v("cp", 0, L), lu), F.Copy, 0.5)
-            act(v(sd_, 96, 192), ind(v("yaw", nxt, nxt + L), lu), F.Copy)
-            sx = send(sd_, "ld%d" % n, 192, "rd%d" % n)
-        else:
-            for k, (a, b) in enumerate(CH):
-                o = P(k, 0, b - a)
-                act(o, v("cp", a, b), F.Sigmoid, -8.0, 240.0)
-                tt(v("oc", a, b), v("cp", a, b), o, A.mult)
-                dma("y", T.yc[:, a:b], T.oc[:, a:b], [v("oc", a, b)], [], 2.2)
-                if k in OPT["KP"]:
-                    o = P(3 + k, 0, b - a)
-                    pe([(o, IDN, act(v("dl", a, b), ind(v("kt", 0, 3328), lst(hu, a, b)), F.Copy), True, True)])
-                    tt(v("oa", a, b), o, v("yaw", nxt + a, nxt + b), A.mult)
-                else:
-                    tt(v("oa", a, b), ind(v("kt", 0, 3328), lst(hu, a, b)), v("yaw", nxt + a, nxt + b), A.mult)
-                dma("y", T.ya[:, a:b], T.oa[:, a:b], [v("oa", a, b)], [], 2.2)
+            act(v("sc%d" % n, 0, 96), ind(v("cp", 0, L), lu), F.Copy, 0.5)
+            sent["c"] = send("sc%d" % n, "lc%d" % n, "rc%d" % n)
+        masked, wide = n in OPT["FM"], 2.0 ** (n + 1)
+        for k, (a, b) in enumerate(CH):
+            dh = ind(v("dt", 0, H + 16), lst(fi, a, b))
+            if masked:
+                o = mm(P(5 + k % 2, 0, b - a), [(Iw[n], act(v("db", a, b), dh, F.Copy)), (FN, v(cr, a, b))])
+                act(v("ff", a, b), o, F.Sigmoid, wide)
+            else:
+                act(v("ff", a, b), dh, F.Sigmoid)
+            tag("f", n)
+            if n == 1 and k == 0:
+                ops[-1]["cost"] += 1.3
+                ops[-1]["hold"] += 1.3
+            tt(v("aq", a, b), ind(v("wa", 0, NA) if n > 1 else v("amb", 0, ARR), lst(ia, a, b)), v("ff", a, b), A.mult)
+            tag("a", n)
+        src, twin = ("aq", "ar") if masked else (cq, cr)
+        if not masked:
+            move("g", v(cq, 0, L), v("aq", 0, L), True)
+        for k, (a, b) in enumerate(CH):
+            copy(OPT["A2"][n - 1][k], v(twin, a, b), v(src, a, b))
+            tt(v("wa", PAD + a, PAD + b), ind(v(src, 0, L + 192 * (n in OPT["AP"])), lst(i2a, a, b)), v(twin, a, b), A.max if masked else A.min)
+            tag("b", n)
+        if n < 3:
+            act(v("sa%d" % n, 0, 96), ind(v("wa", PAD, ARR), lu), F.Copy)
+            sent["a"] = send("sa%d" % n, "la%d" % n, "ra%d" % n)
+    for k, (a, b) in enumerate(CH):
+        tt(v("oa", a, b), ind(v("kt", 0, PAD + H), lst(hu, a, b)), v("wa", PAD + a, PAD + b), A.mult)
+        dma("y", T.ya[:, a:b], T.oa[:, a:b], [v("oa", a, b)], [], 4 * (b - a))
+        o = mm(P(5 + k % 2, 0, b - a), [(I20, act(v("dd", a, b), v("oa", a, b), F.Sign))])
+        tt(v("oc", a, b), v("cp", a, b), o, A.mult)
+        dma("y", T.yc[:, a:b], T.oc[:, a:b], [v("oc", a, b)], [], 4 * (b - a))
 
     no = len(ops)
     succ = [[] for _ in range(no)]
     for i, o in enumerate(ops):
         o["pre"] = [(j, LAT) for j in o["deps"]] + ([(o["after"], NET)] if o["after"] is not None else [])
+    for a, b in OPT["HINT"]:
+        for i in tags[b]:
+            ops[i]["pre"] += [(j, 0.0) for j in tags[a]]
+    for i, o in enumerate(ops):
         for j, lat in o["pre"]:
             succ[j].append((i, lat))
-    prio = [0.0] * no
-    for i in range(no - 1, -1, -1):
-        prio[i] = ops[i]["cost"] + max([lat + prio[j] for j, lat in succ[i]], default=0.0)
     pred = [o["pre"] for o in ops]
+    cost = [o["cost"] for o in ops]
+    use = []
+    for o in ops:
+        use.append([(o["e"], 0.0, o["hold"], None)] + [(b, 0.0, o["cost"] + LAT, o["e"]) for b in o["banks"]])
+        if o["bw"]:
+            use[-1].append(("dma", o["cost"] - o["bw"] - 0.5, o["bw"], None))
+    back = [[(r, cost[i] - a - d, d, e) for r, a, d, e in use[i]] for i in range(no)]
 
-    def place(pr, before, behind, back):
-        left, ready, start = [len(x) for x in before], [0.0] * no, [0.0] * no
+    def place(seq, before, uses):
+        start, busy = [0.0] * no, {}
+        for i in seq:
+            t0 = max([start[j] + cost[j] + lat for j, lat in before[i]], default=0.0)
+            moved = True
+            while moved:
+                moved = False
+                for r, a, d, e in uses[i]:
+                    lane = busy.setdefault(r, [])
+                    k = len(lane)
+                    while k and lane[k - 1][1] > t0 + a - 3.0:
+                        k -= 1
+                    for x, y, e2 in lane[k:]:
+                        if x >= t0 + a + d - 1e-9:
+                            break
+                        if y > t0 + a + 1e-9 and (e is None or e != e2):
+                            t0, moved = y - a, True
+            for r, a, d, e in uses[i]:
+                lane = busy[r]
+                k = len(lane)
+                while k and lane[k - 1][0] > t0 + a:
+                    k -= 1
+                lane.insert(k, (t0 + a, t0 + a + d, e))
+            start[i] = t0
+        return start, max(start[i] + cost[i] for i in range(no))
+
+    def ranked(pr, before, behind):
+        left, out = [len(x) for x in before], []
         cand = [i for i in range(no) if left[i] == 0]
-        busy = {e: 0.0 for e in "vspgy"}
-        off = [o["cost"] - o["hold"] if back else 0.0 for o in ops]
         while cand:
-            i = min(cand, key=lambda i: (max(busy[ops[i]["e"]], ready[i] + off[i]), -pr[i]))
-            e = ops[i]["e"]
-            lim = max(busy[e], ready[i] + off[i]) + OPT["AL"] * ops[i]["hold"]
-            i = max([j for j in cand if ops[j]["e"] == e and ready[j] + off[j] <= lim], key=lambda j: pr[j])
+            i = max(cand, key=lambda j: pr[j])
             cand.remove(i)
-            o = ops[i]
-            t0 = max(busy[e], ready[i] + off[i])
-            busy[e] = t0 + o["hold"]
-            start[i] = t0 - off[i]
+            out.append(i)
             for j, lat in behind[i]:
-                ready[j] = max(ready[j], start[i] + o["cost"] + lat)
                 left[j] -= 1
                 if left[j] == 0:
                     cand.append(j)
-        return start, max(start[i] + ops[i]["cost"] for i in range(no))
+        return out
 
-    key = str(sorted(OPT.items())) + str((CY, GC, SC, LAT, PC, DM, NET, OV))
+    key = str(sorted(OPT.items())) + str((CY, GC, SC, LAT, PC, DM, NET, OV, BW, GH))
     if key not in KEPT:
-        seed, best = OPT["SEED"], None
+        seed, prio, cur, best = [OPT["SEED"]], [-float(i) for i in range(no)], None, None
+
+        def rnd():
+            seed[0] = (seed[0] * 1103515245 + 12345) % 2147483648
+            return seed[0] / 2147483648
+
         for it in range(OPT["IT"]):
-            start, end = place(prio, pred, succ, False)
+            start, end = place(ranked(prio, pred, succ), pred, use)
+            aim = end + OPT["MW"] * sum(start[i] for n in "123" for i in tags["x" + n])
+            if cur is None or aim < cur[0] + OPT["AL"] * (1 - it / OPT["IT"]) * rnd():
+                cur = (aim, start)
             if best is None or end < best[0]:
                 best = (end, start)
-            rstart = place([start[i] + ops[i]["cost"] for i in range(no)], succ, pred, True)[0]
-            prio = []
-            for i in range(no):
-                seed = (seed * 1103515245 + 12345) % 2147483648
-                prio.append(rstart[i] + ops[i]["cost"] + OPT["NZ"] * seed / 2147483648)
-        KEPT[key] = best[1]
+            fin = [cur[1][i] + cost[i] + OPT["NZ"] * rnd() for i in range(no)]
+            for _ in range(OPT["KICK"]):
+                a, w, s = int(rnd() * no), int(rnd() ** 2 * 40) + 1, (rnd() - 0.5) * OPT["KW"]
+                e = ops[a]["e"] if rnd() < 0.5 else None
+                for i in range(a, min(no, a + w)):
+                    if e in (None, ops[i]["e"]):
+                        fin[i] += s
+            rstart = place(ranked(fin, succ, pred), succ, back)[0]
+            prio = [rstart[i] + cost[i] for i in range(no)]
+        seq = sorted(range(no), key=lambda i: (best[1][i], i))
+        eng, hold = [o["e"] for o in ops], [o["hold"] for o in ops]
+        banks, bw = [o["banks"] for o in ops], [o["bw"] for o in ops]
+        marks = [tags["x" + n][0] for n in "123"]
+
+        cases = []
+        for fe, fd in OPT["CASES"]:
+            cases.append(([c * (fd if o["sem"] else fe) for c, o in zip(cost, ops)],
+                          [h * (fd if o["sem"] else fe) for h, o in zip(hold, ops)], [x * fd for x in bw],
+                          [[(j, lat * (fd if lat == NET else 1)) for j, lat in x] for x in pred]))
+
+        def timed(seq):
+            out = [timed1(seq, *c) for c in cases]
+            pick = out[int(rnd() * len(out))]
+            n = len(out)
+            return sum(x[0] for x in out) / n, sum(x[1] for x in out) / n, pick[2], pick[3], pick[4]
+
+        def timed1(seq, cost, hold, bw, pred):
+            fin, start, why, busy, turn, lane = [0.0] * no, [0.0] * no, [None] * no, {}, {}, (0.0, None)
+            for i in seq:
+                e = eng[i]
+                t0, w = busy.get(e, (0.0, None))
+                for j, lat in pred[i]:
+                    if fin[j] + lat > t0:
+                        t0, w = fin[j] + lat, ~j
+                for b in banks[i]:
+                    x = turn.get(b)
+                    if x:
+                        f, j = x[0] if x[2] != e else x[1]
+                        if f > t0:
+                            t0, w = f, j
+                f = t0 + cost[i]
+                if bw[i]:
+                    if lane[0] + bw[i] + 0.5 > f:
+                        f, w = lane[0] + bw[i] + 0.5, lane[1]
+                    lane = (f - 0.5, i)
+                for b in banks[i]:
+                    x = turn.get(b)
+                    turn[b] = ((f + LAT, i), (x[0] if x[2] != e else x[1]) if x else (0.0, None), e)
+                busy[e], fin[i], start[i], why[i] = (t0 + hold[i], i), f, t0, w
+            end = max(fin)
+            return end + OPT["MW"] * sum(start[i] for i in marks), end, start, why, fin.index(end)
+
+        def moved(seq, a, b, up):
+            part = seq[a:b + 1]
+            if up:
+                part.reverse()
+            need, go, rest = {part[0]}, [], []
+            for k in part:
+                if k in need:
+                    go.append(k)
+                    need.update(x for x, lat in (pred if up else succ)[k])
+                else:
+                    rest.append(k)
+            part = go[::-1] + rest[::-1] if up else rest + go
+            return seq[:a] + part + seq[b + 1:]
+
+        cur = timed(seq)
+        best = (cur[1], seq, cur[2])
+        for it in range(OPT["LS"]):
+            i, held = cur[4] if rnd() > OPT["LM"] else marks[int(rnd() * 3)], []
+            while cur[3][i] is not None:
+                j = cur[3][i]
+                if j >= 0:
+                    held.append((j, i))
+                i = j if j >= 0 else ~j
+            if held and rnd() < OPT["LC"]:
+                j, i = held[int(rnd() * len(held))]
+                a, b = max(0, seq.index(j) - int(rnd() ** 3 * OPT["LW"])), seq.index(i)
+            else:
+                a = int(rnd() * (no - 1))
+                b = min(no - 1, a + 1 + int(rnd() ** 2 * 2 * OPT["LW"]))
+            s2 = moved(seq, a, b, rnd() < 0.5)
+            c2 = timed(s2)
+            if c2[0] <= cur[0] + OPT["LT"] * (1 - it / OPT["LS"]) * rnd() ** 2:
+                seq, cur = s2, c2
+                if cur[1] < best[0]:
+                    best = (cur[1], seq, cur[2])
+        KEPT[key] = best
+    order = KEPT[key][1]
     for i in range(no):
-        ops[i]["t"] = KEPT[key][i]
-    order = sorted(range(no), key=lambda i: (ops[i]["t"], i))
+        ops[i]["t"] = KEPT[key][2][i]
+    last = {}
+    for i in order:
+        for b in ops[i]["banks"]:
+            ops[i]["deps"].update(j for e, j in last.setdefault(b, {}).items() if e != ops[i]["e"])
+            last[b][ops[i]["e"]] = i
+        if ops[i]["scatter"]:
+            ops[i]["deps"].update(last.get("scatter", []))
+            last["scatter"] = [i]
 
     queue = {"v": g.vector, "s": g.scalar, "p": g.tensor, "g": g, "y": g.sync}
     esem = {"v": "sv", "s": "ss", "p": "sp", "g": "sg"}

from concourse.bass import DstId, RemoteDMATransfer
from concourse.mybir import AluOpType as A, ActivationFunctionType as F

L, H, H0 = 1280, 3072, 2816
PAD = 16
ARR, OL, OR = PAD + L, 13 * 128, 23 * 128
NA, NC = ARR + 384, PAD + OR + L
XD, XF, XP, NX, NZ = 1296, 1680, 2960, 3712, 1024
BIG = 4096.0
HS = BIG - 1024 - 3.5
M8 = 1.5 * 2.0 ** 26
TS = BIG - XF
CH = [(0, 448), (448, 864), (864, 1280)]
NW, NB, NU, NI = 8192, 8192, 1536, 1280

SCRATCH = {
    "kt": ("sbuf", [128, PAD + H], "bfloat16"), "dt": ("sbuf", [128, H + 16], "bfloat16"),
    "tab": ("sbuf", [128, PAD + 2 * H], "bfloat16"), "cw": ("sbuf", [128, NC], "float32"),
    "wa": ("sbuf", [128, NA], "float32"), "idc": ("sbuf", [128, 1664], "bfloat16"),
    "xw": ("sbuf", [128, NX], "bfloat16"), "zz": ("sbuf", [128, NZ], "bfloat16"), "ones": ("sbuf", [128, 192], "bfloat16"),
    "w": ("sbuf", [128, NW], "float32"), "wb": ("sbuf", [128, NB], "bfloat16"),
    "wu": ("sbuf", [128, NU], "uint16"), "wi": ("sbuf", [128, NI], "int32"),
    "vl": ("sbuf", [128, 2 * L], "bfloat16"),
}
SCRATCH["aq"] = ("sbuf", [128, L + 192], "float32")
SCRATCH["amb"] = ("sbuf", [128, ARR], "bfloat16")
for _n in ("crb", "crc", "rr", "dd", "gx", "xg", "kb", "db"):
    SCRATCH[_n] = ("sbuf", [128, L], "bfloat16")
for _n in ("cp", "cq0", "cq1", "cr0", "cr1", "ar", "ff", "oc", "oa"):
    SCRATCH[_n] = ("sbuf", [128, L], "float32")
for _n in ("1", "2"):
    SCRATCH["sh" + _n] = ("sbuf", [128, 96], "bfloat16")
    SCRATCH["lh" + _n] = ("sbuf", [128, 192], "bfloat16")
    for _k in "ca":
        SCRATCH["s" + _k + _n] = ("sbuf", [128, 96], "float32")
        SCRATCH["l" + _k + _n] = ("sbuf", [128, 192], "float32")
for _b in range(8):
    SCRATCH["p%d" % _b] = ("psum", [128, 512], "float32")
NDMA = 80
SEMAPHORES = ["sv", "ss", "sp", "sg", "sent", "rh1", "rh2", "rc1", "rc2", "ra1", "ra2"] + ["d%d" % _i for _i in range(NDMA)]
TWO = [_n for _n in SCRATCH if SCRATCH[_n][2] in ("bfloat16", "uint16")]
CY = 0.83e-3 * 1.2
GC, SC, LAT, NET, OV = 1.56, 3.8, 0.13, 3.5, 0.05
PC, DM, BW, GH = 0.5e-3, 1.1, 9 / 38e3, 1.0
OPT = {"XS": (768, 768, 768), "CS": (768, 768, 768), "XC": (0, 640, 1280), "VS": ((1, 0), (1, 1), (2, 0), (2, 1), (3, 0), (3, 1)),
       "C2": ("syy",) * 3, "A2": ("yyy", "yyy", "sss"), "FM": (2, 3), "TP": (), "PA": ((0, L),) * 3, "HS": 2 ** 30 - 1 - 2 ** 11, "TI": "vvvsss",
       "AP": (3,), "XI": "yyyyyy", "DV": (), "KG": 2 ** 40 - 1, "TQ": "ysysysysys",
       "HINT": (("t1", "x1"), ("t2", "x2"), ("t3", "x3"), ("o2", "f1"), ("o3", "f2")), "AL": 0.3, "IT": 300, "SEED": 764, "NZ": 0.1, "KICK": 2, "KW": 10, "MW": 0.1,
       "CASES": ((0.85, 1.0), (1.15, 1.0)), "LS": 24000, "LT": 0.2, "LC": 0.6, "LM": 0.4, "LW": 20}
KEPT = {}


def rank_program(g, core, T, topo):
    rank = T.rank_of(core)
    if rank is None:
        return
    nr = len(T.cores)
    ops, acc, top, names = [], {}, {"w": 0, "wb": 0, "wu": 0, "wi": 0}, {}

    def v(name, a, b, s=1):
        return (name, a, b, s)

    def new(buf, n=80):
        a = top[buf]
        top[buf] = a + (n + 15) // 16 * 16
        assert top[buf] <= SCRATCH[buf][1][1]
        return (buf, a, a + n, 1)

    def sub(x, a, b, s=1):
        return (x[0], x[1] + a, x[1] + b, s)

    def ind(win, off):
        return ("ind", win, off)

    def ap(x):
        if not isinstance(x, tuple):
            return x
        if x[0] == "ind":
            return ap(x[1]).indirect(ap(x[2]))
        return T[x[0]][:, x[1]:x[2]] if x[3] == 1 else T[x[0]][:, x[1]:x[2]:x[3]]

    def cnt(x):
        return 16 * cnt(x[2]) if x[0] == "ind" else (x[2] - x[1] + x[3] - 1) // x[3]

    def psum(x):
        return x[0][0] == "p" and x[0][1:].isdigit()

    def op(eng, fn, R, W, cost, hold=None, sem=None, xw=None, after=None, bw=0.0):
        rs, ws = [], []
        for x in R:
            if isinstance(x, tuple):
                rs += [x[1], x[2]] if x[0] == "ind" else [x]
        for x in W:
            if x[0] == "ind":
                ws.append(x[1])
                rs.append(x[2])
            else:
                ws.append(x)
        me, deps = len(ops), set()
        scatter = any(x[0] == "ind" for x in W)
        for x, w in [(x, False) for x in rs] + [(x, True) for x in ws]:
            for (j, a, b, w2) in acc.setdefault(x[0], []):
                if (w or w2) and a < x[2] and x[1] < b and not (scatter and ops[j]["scatter"]):
                    deps.add(j)
        for x, w in [(x, False) for x in rs] + [(x, True) for x in ws]:
            acc[x[0]].append((me, x[1], x[2], w))
        ops.append({"e": eng, "fn": fn, "deps": deps, "cost": cost, "hold": cost if hold is None else hold, "sem": sem,
                    "banks": sorted({x[0] for x in rs + ws if psum(x) and x[0] != "p7"}), "bw": bw, "scatter": scatter,
                    "xw": xw, "after": after})
        return me

    tags = {}

    def tag(name, n):
        tags.setdefault(name + str(n), []).append(len(ops) - 1)

    def vcost(o, xs, two=False):
        n = cnt(o)
        if o[0] == "ind":
            return 0.05 + n * SC * CY
        if any(isinstance(x, tuple) and x[0] == "ind" for x in xs):
            return 0.05 + n * GC * CY
        if two:
            f = 1.0 if any(psum(x) for x in xs) else 2.0
        else:
            f = 0.5 if o[0] in TWO and xs[0][0] in TWO else 1.0
        return OV + max(64, n * f) * CY

    def tt(o, a, b, f, extra=()):
        op("v", lambda: g.vector.tensor_tensor(ap(o), ap(a), ap(b), f), [a, b] + list(extra), [o], vcost(o, [a, b], True))
        return o

    def ts(o, a, s1, f1, s2=None, f2=None, xw=None, after=None):
        if f2 is None:
            fn = lambda: g.vector.tensor_scalar(ap(o), ap(a), ap(s1), None, f1)
        else:
            fn = lambda: g.vector.tensor_scalar(ap(o), ap(a), ap(s1), ap(s2), f1, f2)
        op("v", fn, [a, s1, s2], [o], vcost(o, [a]), xw=xw, after=after)
        return o

    def cp(o, a):
        op("v", lambda: g.vector.tensor_copy(ap(o), ap(a)), [a], [o], vcost(o, [a]))
        return o

    def fill(o, c):
        op("v", lambda: g.vector.memset(ap(o), c), [], [o], OV + max(64, cnt(o) * (0.5 if o[0] in TWO else 1)) * CY)
        return o

    def scan(o, a):
        one = v("ones", 0, cnt(a))
        op("v", lambda: g.vector.tensor_tensor_scan(ap(o), ap(one), ap(a), 0.0, A.mult, A.add), [a, one], [o], vcost(o, [a]))
        return o

    def act(o, a, f, scale=1.0, bias=None, accum=None, extra=(), xw=None, after=None):
        kw = {"scale": ap(scale)}
        if bias is not None:
            kw["bias"] = ap(bias)
        if accum is not None:
            kw["accum_out"] = ap(accum)
        c = 0.065 + cnt(o) * GC * CY if a[0] == "ind" else OV + max(64, cnt(o)) * CY + (0.02 if accum else 0)
        op("s", lambda: g.scalar.activation(ap(o), ap(a), f, **kw), [a, scale, bias] + list(extra),
           [o] + ([accum] if accum else []), c, xw=xw, after=after)
        return o

    def lin(o, a, scale, bias):
        return act(o, a, F.Identity, scale, bias)

    def pe(items, xw=None, after=None):
        def fn():
            last = None
            for (o, l, r, st, sp) in items:
                last = g.tensor.matmul(ap(o), ap(l), ap(r), st, sp)
            return last
        op("p", fn, [x[1] for x in items] + [x[2] for x in items], [x[0] for x in items],
           0.05 + sum(max(64, cnt(x[2])) * (1 if x[2][0] in TWO else 4) * PC for x in items), xw=xw, after=after)

    def mm(o, terms, convs=(), late=(), xw=None, after=None):
        items = list(terms)
        for B, src in convs:
            items += [(sub(B, 15 - i, 143 - i), sub(src, i, cnt(src), 16)) for i in range(16)]
        pe([(o, l, r, i == 0, i == len(items) - 1 and not late) for i, (l, r) in enumerate(items)], xw, after)
        if late:
            pe([(o, l, r, False, i == len(late) - 1) for i, (l, r) in enumerate(late)])
        return o

    def iota(o, pat, base, mul):
        if o[0] == "wi":
            fn = lambda: g.iota(ap(o), pat, base, mul)
        else:
            fn = lambda: g.iota(ap(o), pat, base, mul, allow_small_or_imprecise_dtypes=True)
        op("g", fn, [], [o], 0.13 + 2 * cnt(o) * CY)
        return o

    def select(o, a, pat, f, c, base, mul):
        op("g", lambda: g.affine_select(ap(o), ap(a), pat, f, c, base, mul), [a], [o], 0.17 + 2 * cnt(o) * CY)
        return o

    nd = [0]

    def dma(eng, out, in_, R, W, size, add=False):
        q = {"y": g.sync, "s": g.scalar, "g": g}[eng]
        s = "d%d" % nd[0]
        nd[0] += 1
        kw = {"accum_op": A.add} if add else {}
        bw = size * (2 if add else 1) * BW
        op(eng, lambda: q.dma_start(out, in_, **kw), R, W, (2.4 if eng == "g" else 2.0) * DM + bw,
           hold=GH if eng == "g" else 0.1, sem=s, bw=bw)

    def move(eng, o, a, add=False):
        dma(eng, ap(o), ap(a), [a] + ([o] if add else []), [o], cnt(o) * (2 if o[0] in TWO else 4), add)

    def copy(eng, o, a):
        if eng == "s":
            act(o, a, F.Copy)
        elif eng == "v":
            cp(o, a)
        else:
            move(eng, o, a)

    def send(src, land, sem):
        trs = []
        for k, step in enumerate((1, 3)):
            dst = T.cores[(rank + step) % nr]
            rid, pid = topo.addr(dst)[:2]
            eng = topo.engines(core, dst)
            half = len(eng) // 2
            m = sum(1 << e for e in eng[k * half:(k + 1) * half])
            trs.append(RemoteDMATransfer(dst_ids=[DstId(rid=rid, pnc=pid)], dma_engine_mask=m, remote_sem=T.sem[sem],
                                         src=T[src][:], dst=T[land][:, k * 96:(k + 1) * 96]))
            names["sent"] = names.get("sent", 0) + half
            names[sem] = names.get(sem, 0) + half
        return op("g", lambda: g.remote_dma_fused(trs, local_sem=T.sem.sent), [v(src, 0, 96)], [], 0.5, sem="none")

    W = lambda n=80: new("w", n)
    Bf = lambda n=80: new("wb", n)
    U = lambda n=80: new("wu", n)
    I32 = lambda n=80: new("wi", n)
    P = lambda b, a, c: v("p%d" % b, a, c)
    Q = lambda k, n=80: v("p7", 80 * k, 80 * k + n)
    lst = lambda x, a, b: sub(x, a // 16, b // 16)

    pli, exi = I32(80), I32(352)
    dma("s", ap(sub(exi, 0, 176)), T.lf[:, 0:H0], [], [sub(exi, 0, 176)], 704)
    dma("y", ap(sub(exi, 176, 352)), T.rt[:, 0:H0], [], [sub(exi, 176, 352)], 704)
    dma("s", ap(pli), T.place[:], [], [pli], 320)
    dma("y", T.amb[:, PAD:ARR], T.amp[:], [], [v("amb", PAD, ARR)], 2 * L)
    dma("y", T.crb[:], T.cro[:], [], [v("crb", 0, L)], 2 * L)
    dma("y", T.crc[:], T.cro[:], [], [v("crc", 0, L)], 2 * L)
    dma("y", T.kt[:, PAD:PAD + H0], T.kap[:, 0:H0], [], [v("kt", PAD, PAD + H0)], 2 * H0)
    dma("y", T.dt[:, 0:H], T.dam[:], [], [v("dt", 0, H)], 2 * H)

    pi = iota(I32(1), [[0, 1]], 0, 1)
    xrow = iota(W(144), [[1, 144]], -15, 0)
    g16 = iota(W(128), [[16, 8], [0, 16]], 0, 0)
    ownp = iota(W(80), [[16, 80]], 0, 1)
    zz = fill(v("zz", 0, NZ), 0.0)
    zf = iota(W(128), [[0, 128]], 0, 0)
    nk = [0]

    def const(o, c):
        nk[0] += 1
        if not OPT["KG"] >> nk[0] & 1:
            return fill(o, c)
        if c == int(c):
            return iota(o, [[0, cnt(o)]], int(c), 0)
        return select(o, sub(zz, 0, cnt(o)), [[0, cnt(o)]], A.is_gt, c, 0, 0)

    def zero(e, o):
        if e == "v":
            fill(o, 0.0)
        elif e == "g":
            iota(o, [[0, cnt(o)]], 0, 0)
        else:
            copy(e, o, sub(zz, 0, cnt(o)))

    def ident(c, buf="wb"):
        nk[0] += 1
        if OPT["KG"] >> nk[0] & 1:
            return select(new(buf, 128), sub(zz, 0, 128) if buf == "wb" else zf, [[-1, 128]], A.not_equal, c, 0, 1)
        return ts(new(buf, 128), IDN if buf == "wb" else IDF, c, A.mult)

    for k in range(2):
        for j, (a, b) in enumerate(((0, NZ), (NZ, 2 * NZ), (2 * NZ, H))):
            zero(OPT["TI"][3 * k + j], v("tab", PAD + k * H + a, PAD + k * H + b))
    for k, o in enumerate([v("xw", a, min(NX, a + NZ)) for a in range(0, NX, NZ)] + [v("idc", 0, NZ), v("idc", NZ, 1664)]):
        zero(OPT["XI"][k], o)
    const(v("ones", 0, 192), 1.0)
    const(v("kt", 0, PAD), 0.0)
    const(v("kt", PAD + H0, PAD + H), 0.5)
    const(v("dt", H, H + 16), 20.0)
    const(v("amb", 0, PAD), 0.0)
    c8, c35 = const(Bf(), 8.0 / BIG), const(Bf(), -3.5)
    pf = cp(W(1), pi)
    pm = cp(W(1), ts(I32(1), pi, 15, A.bitwise_and))
    t16 = ts(I32(1), pi, 16, A.bitwise_and)
    me_ = ts(W(1), t16, 0.0, A.is_equal)
    mo_ = ts(W(1), t16, 0.0, A.is_gt)
    pg = tt(W(1), pf, pm, A.subtract)
    mrow, j1 = sub(xrow, 15, 143), sub(xrow, 16, 112)
    oh = ts(W(16), sub(xrow, 15, 31), pm, A.is_equal)
    OH = lambda j: sub(oh, j, j + 1)
    B0 = ts(Bf(144), xrow, pg, A.is_equal)
    own = ts(W(), ownp, pg, A.subtract)
    ONES = ts(Bf(128), g16, pg, A.is_equal)
    IDN = ts(Bf(128), mrow, pf, A.is_equal)
    IDF = ts(W(128), mrow, pf, A.is_equal)
    NUT = tt(Bf(128), ts(Q(0, 128), mrow, pf, A.is_le, -1.0, A.mult), ONES, A.mult)

    def col(terms, c=None):
        for j, wgt in terms:
            c = act(W(1), OH(j), F.Identity, float(wgt), c)
        return c

    def scaled(src, c, buf="wb"):
        return act(new(buf, cnt(src)), src, F.Copy, c)

    nh = [0]

    def half(src, c):
        nh[0] += 1
        return scaled(src, c) if OPT["HS"] >> nh[0] & 1 else ts(Bf(cnt(src)), src, c, A.mult)

    wid = col([(2, 104)], OH(3))
    w0, w8 = col([(0, 8)]), col([(8, 8)])
    Bhw, Boj, Boc = [half(B0, c) for c in (col([(0, 8)], OH(4)), w8, col([(1, 128)]))]
    Bc, Bt, Bh = [half(B0, c) for c in (col([(5, OL + OR), (1, -128)], wid), wid, col([(8, 8)], OH(12)))]
    Bjp = half(B0, col([(5, BIG)], w0))
    cm8 = const(Bf(), M8 / BIG)
    B32, B128, Bpm = half(B0, 1 / 32), half(B0, BIG / 32), half(B0, pm)
    Bd = {1: half(B0, -2.0 ** -23), 2: half(B0, -0.5)}
    O32 = half(ONES, 1 / 32)
    Ip, In, I15, Il, Ir, I256, I20 = [ident(c) for c in (BIG, -BIG, H / 2, -OL / 2, (OL - OR) / 2, 256.0, 2.0 ** 20)]
    F128, FN = ident(-128.0, "w"), ident(-1.0, "w")
    Iw = {n: ident(2.0 ** (-n - 1)) for n in OPT["FM"]}
    jb = lin(W(6), sub(own, 0, 6), -1.0, -0.5)
    owns = lin(W(), own, 1.0, PAD + TS)
    ownf, cmpw = W(160), W(160)
    lin(sub(ownf, 0, 80), own, 1.0, XF - XP + BIG)
    lin(sub(ownf, 80, 160), own, 1.0, XP - XF + BIG)
    lin(sub(cmpw, 0, 80), own, 1.0, PAD - XP + BIG)
    tws = const(sub(cmpw, 80, 160), TS)
    pgn0 = lin(W(1), pg, 1.0, 16.0)
    pgn = tt(W(1), pgn0, ts(W(1), pgn0, 128.0, A.is_ge, 128.0, A.mult), A.subtract)
    SHO = ts(Bf(128), g16, pgn, A.is_equal, -1.0, A.mult)
    SHF = ts(W(128), mrow, lin(W(1), pgn, 1.0, pm), A.is_equal)
    cs = lin(W(12), sub(own, 0, 12), 1.0, XD - XP + 1 + BIG / 2)
    jh = lin(W(12), sub(own, 0, 12), 0.5, 0.5)
    abase = col([(8, -128), (5, -1)])
    asc = [col([(12, 2)]), col([(12, -2)])]
    abi = [col([(12, -1)], abase), col([(12, 256)], abase)]

    idr = []
    for row, src in ((2, act(Bf(104), v("ones", 0, 104), F.Copy, pm)), (3, iota(Bf(104), [[1, 104]], PAD, 0)), (5, v("ones", 0, 104))):
        idr.append(v("idrow%d" % row, 0, 1))
        dma("y", T.idc[row:128:16, :], ap(src), [src, v("idc", 0, 1664)], [idr[-1]], 500)

    hl, hlb = I32(704), Bf(704)
    ts(sub(hlb, 0, 352), ts(sub(hl, 0, 352), exi, 3, A.arith_shift_right), -128.0, A.add)
    cp(sub(hlb, 352, 704), ts(sub(hl, 352, 704), exi, 7, A.bitwise_and))
    codes = [const(Bf(176), float(c // 128)) for c in (OL, OR)]
    doors = [lin(Bf(16), iota(W(16), [[1, 2], [0, 8]], H0 // 8 - 128, 0), 1.0, lin(W(1), pm, 2.0, 0.0)),
             iota(Bf(16), [[0, 2], [1, 8]], 0, 0)]
    tabr = []
    for k in range(2):
        t0 = PAD + k * H
        rows = [(0, 176 * k), (8, 176 - 176 * k), (4, 352 + 176 * k), (12, 528 - 176 * k)]
        for j, (row, src) in enumerate([(r, sub(hlb, a, a + 176)) for r, a in rows] + [(1, codes[k])]):
            tabr.append(v("tabrow%d_%d" % (k, row), 0, 1))
            dma(OPT["TQ"][5 * k + j], T.tab[row:128:16, t0:t0 + H0], ap(src), [src, v("tab", t0, t0 + H0)], [tabr[-1]], 800)
        for row, src in zip((0, 4), doors):
            tabr.append(v("tabdoor%d_%d" % (k, row), 0, 1))
            dma("y", T.tab[row:128:16, t0 + H0:t0 + H], ap(src), [src, v("tab", t0 + H0, t0 + H)], [tabr[-1]], 200)
    act(v("tab", 0, PAD), v("ones", 0, PAD), F.Copy, col([(0, -129), (1, -16)]))

    plf, pin, pout, hs = ts(W(), pli, HS, A.add), W(160), W(160), W()
    for u in range(5):
        ts(sub(pin, 32 * u, 32 * u + 16), sub(plf, 16 * u, 16 * u + 16), me_, A.mult)
        act(sub(pin, 32 * u + 16, 32 * u + 32), sub(plf, 16 * u, 16 * u + 16), F.Copy, mo_)
    op("v", lambda: g.vector.transpose(ap(pout), ap(pin)), [pin], [pout], 0.19)
    for u in range(5):
        tt(sub(hs, u, 80, 5), sub(pout, 32 * u, 32 * u + 16), sub(pout, 32 * u + 16, 32 * u + 32), A.add)

    ts(v("dd", 0, L), v("amb", PAD, ARR), 0.0, A.is_equal, 2.0 ** 23, A.mult)
    move("g", v("crc", 0, L), v("dd", 0, L), True)
    for k, (a, b) in enumerate(CH):
        o = mm(P(5 + k % 2, 0, b - a), [(IDN, v("crb", a, b)), (IDN, v("dd", a, b))])
        act(v("rr", a, b), o, F.Sign, -1.0, -2.0 ** -40)
    for buf in ("cw", "wa"):
        const(v(buf, 0, PAD), 0.0)
        for a in range(ARR, NA, 128):
            move("y", v(buf, a, a + 128), zf)
    zw, hz = W(96), W(96)
    const(sub(zw, 80, 96), 0.0)
    const(sub(hz, 80, 96), 0.0)

    hu, giu, puw, pur, ic, kcu, apu = U(), U(), U(), U(), U(), U(6), U(12)
    non, stay, sent = None, None, {}
    tmp = {}

    def t_(name, n=80, buf="w"):
        if name not in tmp:
            tmp[name] = new(buf, n)
        return tmp[name]

    rr, dd, gx, xg, xwin = v("rr", 0, L), v("dd", 0, L), v("gx", 0, L), v("xg", 0, L), v("xw", 0, NX)
    ts(hu, hs, PAD - HS, A.add)
    for n in (1, 2, 3):
        lam, mk = ((0.5, 2.0 ** 22), (2.0 ** -19, 16.0), (2.0 ** -20, 8.0))[n - 1]
        ia, i2, fi, lu = U(), U(), U(), U(6)
        if n == 1:
            stay, vb = [(Ip, ts(Bf(), hs, H0 + HS, A.is_ge))], 16.0
        else:
            vb = 16.0 + BIG
        np_ = mm(P(1, 0, 80), [(Ip, c8)] * (2 if n == 1 or n in OPT["DV"] else 1), [(Bd[min(n, 2)], dd)])
        nb = act(t_("nb", 80, "wb"), np_, F.Copy, 1 / BIG)
        vp = mm(P(0, 0, 80), [], [(B0, rr)], stay + [(In, nb)])
        if n == 1:
            non = ts(t_("non", 80, "wb"), np_, 0.5, A.is_gt, -1.0, A.mult)
        av = act(t_("av"), vp, F.Abs, 1.0, vb)
        sgn = act(t_("sgn", 80, "wb"), vp, F.Sign, 1.0, vb - 0.5)
        ts(giu, mm(P(4, 0, 80), [(IDF, hs), (In, non), (In, non), (I15, sgn)]), PAD - HS + H / 2 - 2 * BIG, A.add)
        XC = OPT["XC"]
        for a, b in zip(XC, XC[1:]):
            act(v("gx", a, b), ind(v("tab", 0, PAD + 2 * H), lst(giu, a, b)), F.Copy, extra=tabr)
            tag("g", n)
        sn = scan(t_("sn", 80, "wb"), non)
        fp = P(2, 0, 160)
        for a in (0, 80):
            mm(sub(fp, a, a + 80), [(IDF, sub(ownf, a, a + 80)), (ONES, sn), (NUT, non), (Ip, non), (Ip, non)])
        nfb = lin(t_("nfb", 1), mm(P(2, 160, 161), [(ONES, sub(sn, 79, 80))]), -1.0, BIG - L + 0.5)
        p0 = tt(t_("p0", 160), fp, cmpw, A.max)
        more = []
        if n > 1:
            lhn, got = "lh%d" % (n - 1), ("rh%d" % (n - 1), names["rh%d" % (n - 1)])
            ha = P(3, 0, 192)
            pe([(sub(ha, 0, 96), ONES, v(lhn, 0, 96), True, True), (sub(ha, 96, 192), SHO, v(lhn, 96, 192), True, True)],
               xw=got, after=sent["h"])
            va = act(t_("va", 192, "wb"), ha, F.Sign, 1.0, -0.25, accum=t_("msum", 1))
            ap0 = t_("ap0", 192, "wb")
            for k in range(2):
                lin(sub(ap0, 96 * k, 96 * k + 96), sub(ha, 96 * k, 96 * k + 96), asc[k], abi[k])
            sa = scan(t_("sa", 192, "wb"), va)
            more = [(O32, lin(t_("mrep", 80, "wb"), v("ones", 0, 80), 192.0, t_("msum", 1)))]
            pv = mm(P(3, 192, 204), [(IDF, jh)], [(B128, va), (B32, sa)])
            ts(apu, tt(Q(4, 12), pv, cs, A.max), XP - 1 - BIG / 2, A.add)
            a0 = L + 192 * (n - 2)
            tt(ind(xwin, apu), ap0, v("idc", a0, a0 + 192), A.add, idr)
        dis = tt(t_("dis", 80, "wb"), np_, av, A.is_gt)
        sd = scan(t_("sd", 80, "wb"), dis)
        rank_d = more + [(NUT, dis), (ONES, sd)]
        sgm = act(t_("sgm", 80, "wb"), mm(P(3, 208, 288), [(In, dis)] + rank_d), F.Sign, 1.0, nfb)
        cm = mm(P(1, 320, 400), rank_d + [(In, sgm)])
        ts(puw, tt(Q(0), cm, sub(p0, 0, 80), A.max), XP - BIG, A.add)
        for a, b in zip(XC, XC[1:]):
            tt(ind(xwin, lst(puw, a, b)), v("gx", a, b), v("idc", a, b), A.add, idr)
            tag("x", n)
        ts(pur, tt(Q(1), cm, sub(p0, 80, 160), A.max), XF - BIG, A.add, XP + 736.0, A.min)
        XS = OPT["XS"][n - 1]
        act(v("xg", 0, XS), ind(xwin, lst(pur, 0, XS)), F.Copy)
        if XS < L:
            cp(v("xg", XS, L), ind(xwin, lst(pur, XS, L)))
        if n < 3:
            for a, b in ((0, NZ), (NZ, ARR), (XP, XP + 736)):
                move("y", v("xw", a, b), sub(zz, 0, b - a))
        t = v("cw", PAD, ARR)
        for k, (a, b) in enumerate(CH):
            kh = ind(v("kt", 0, PAD + H), lst(hu, a, b))
            if (n, k) in OPT["TP"]:
                o = mm(P(5 + k % 2, 0, b - a), [(IDN, act(v("kb", a, b), kh, F.Copy))])
                tt(sub(t, a, b), o, v("cp" if n > 1 else "crc", a, b), A.mult)
            else:
                tt(sub(t, a, b), kh, v("cp" if n > 1 else "crc", a, b), A.mult)
            tag("t", n)
        if n == 3:
            dma("y", T.kt[:, PAD + H0:PAD + H], T.kap[:, H0:H], [], [v("kt", PAD + H0, PAD + H)], 512)
        for k, (off, s1, s2) in enumerate(((OL, mk, mk - lam), (OR, -mk, mk + lam))):
            o, part = v("vl", k * L, k * L + L), v("cw", PAD + off, ARR + off)
            if (n, k) in OPT["VS"]:
                for a, b in CH:
                    lin(sub(part, a, b), sub(rr, a, b), s1, s2)
                    tag("o", n)
                PA = OPT["PA"][n - 1]
                for a, b in zip(PA, PA[1:]):
                    move("g", sub(part, a, b), sub(t, a, b), True)
            else:
                ts(o, rr, s1, A.mult, s2, A.add)
                move("y", part, t)
                move("g", part, o, True)
        if n > 1:
            r0 = ARR + 192 * (n - 2)
            for k, (c, buf) in enumerate((("c", "cw"), ("a", "wa"))):
                ldn, got = "l%s%d" % (c, n - 1), ("r%s%d" % (c, n - 1), names["r%s%d" % (c, n - 1)])
                po = mm(P(2, 256 + 96 * k, 352 + 96 * k), [(SHF, v(ldn, 96, 192))], xw=got, after=sent[c])
                o = v("aq", L, L + 192) if c == "a" and n in OPT["AP"] else v(buf, r0, r0 + 192)
                act(sub(o, 0, 96), v(ldn, 0, 96), F.Copy, xw=got, after=sent[c])
                act(sub(o, 96, 192), po, F.Copy)
        oc = lin(t_("oc"), mm(P(4, 240, 320), [(IDF, owns)], [(Boc, gx)]), 1.0, -TS)
        ojm = lin(t_("ojm"), mm(P(1, 400, 480), [(In, sgm)], [(Boj, gx)]), 1.0, M8)
        hw = lin(t_("hw"), mm(P(4, 320, 400), [], [(Bhw, gx)]), 1.0, HS + 1024)
        icf = tt(t_("icf"), mm(P(0, 80, 160), [(Ip, non), (Ip, non)], [(Bc, xg)]), oc, A.max)
        cp(ic, icf)
        hs = tt(t_("hs%d" % (n % 2)), mm(P(4, 80, 160), [(Ip, non), (Ip, v("ones", 0, 80)), (IDN, c35)], [(Bh, xg)]), hw, A.max)
        js = lin(t_("js"), hs, 1.0, M8)
        jp = tt(Q(2), mm(P(1, 80, 160), [(Ip, cm8)], [(Bjp, xg)]), ojm, A.max)
        ne = tt(t_("ne", 80, "wb"), jp, js, A.not_equal)
        lin(tws, mm(P(3, 288, 368), [], [(Bt, xg)]), 1.0, TS)
        ts(i2, tt(Q(3), mm(P(0, 240, 320), [(IDF, tws), (In, ne)]), owns, A.max), -(PAD + TS), A.add)
        none = act(t_("none", 80, "wb"), icf, F.Relu, -2.0, 2.0)
        on2 = tt(t_("on2", 80, "wb"), mm(P(2, 176, 256), [(IDF, tws), (In, none), (Ip, ne)]), owns, A.is_ge)
        s1, s2 = [act(t_("s%d" % c, 80, "wb"), icf, F.Sign, 1.0, 0.5 - PAD - c) for c in (OL, OR)]
        ts(fi, mm(P(4, 160, 240), [(IDF, hs), (In, s1)]), BIG - HS, A.add, float(H), A.min)
        i2a, drop = i2, []
        if n in OPT["AP"]:
            s0 = act(t_("s0", 80, "wb"), icf, F.Sign, 1.0, 0.5 - ARR)
            ya_ = lin(t_("ya_"), mm(P(0, 320, 400), [(IDF, icf), (Ip, s0), (In, s1)]), 1.0, L - r0 + PAD + TS - 2 * BIG)
            i2a, drop = ts(U(), tt(Q(5), Q(3), ya_, A.max), -(PAD + TS), A.add), [(In, s0), (Ip, s1)]
        ts(ia, mm(P(4, 400, 480), [(IDF, icf), (Il, s1), (Ir, s2)] + drop), -OR / 2, A.add)
        ho = mm(P(0, 160, 240), [(IDF, hs), (Ip, on2)])
        if n < 3:
            lv = ts(t_("lv", 80, "wb"), ho, H0 + HS + BIG, A.is_ge)
            stay = [(In, on2), (Ip, lv)]
            sl = scan(t_("sl", 80, "wb"), lv)
            r1 = mm(P(1, 240, 320), [(ONES, sl)])
            r2 = mm(P(2, 0, 80), [(In, lv), (Ip, on2), (Ip, on2), (NUT, lv), (ONES, sl)])
            sg = t_("sg", 6)
            for c in range(6):
                act(t_("junk%d" % c), r1, F.Sign, 1.0, sub(jb, c, c + 1), accum=sub(sg, c, c + 1))
            lin(sub(zw, 0, 80), r2, 1.0, 1.0 - BIG)
            non = ts(t_("non", 80, "wb"), r2, BIG + 96, A.is_ge, -1.0, A.mult)
            ts(hu, hs, PAD - HS, A.add)
            kb = lin(t_("kb", 80, "wb"), hs, 0.499, 128.0 - 0.499 * (H0 + HS))
            lin(sub(hz, 0, 80), mm(P(3, 368, 448), [(F128, hs), (I256, kb), (IDN, kb)]), 1.0,
                128.0 * (H0 + HS) - 257 * 128 + 0.5)
            ts(kcu, sg, -0.5, A.mult, 40.0, A.add)
            kc16 = lin(t_("kc16", 6), sg, -8.0, 640.0)
            hit = tt(t_("hit", 96, "wb"), ind(zw, kcu), j1, A.is_equal)
            tt(v("sh%d" % n, 0, 96), ind(hz, kcu), hit, A.mult)
            sent["h"] = send("sh%d" % n, "lh%d" % n, "rh%d" % n)
            ts(lu, mm(P(1, 480, 486), [(IDF, kc16)], [(Bpm, hit)]), float(L - 1), A.min)
        else:
            ts(hu, ho, PAD - HS - BIG, A.add)
        CS, sc = OPT["CS"][n - 1], 2.0 ** -17 if n == 1 else 1.0
        cq = "cq%d" % (n % 2)
        for a, b in ((0, CS // 32 * 16), (CS // 32 * 16, CS)):
            act(v(cq, a, b), ind(v("cw", 0, NC), lst(ic, a, b)), F.Copy, sc)
        if CS < L:
            ts(v(cq, CS, L), ind(v("cw", 0, NC), lst(ic, CS, L)), sc, A.mult)
        cr = "cr%d" % (n % 2)
        for k, (a, b) in enumerate(CH):
            copy(OPT["C2"][n - 1][k], v(cr, a, b), v(cq, a, b))
            tt(v("cp", a, b), ind(v(cq, 0, L), lst(i2, a, b)), v(cr, a, b), A.min)
            tag("c", n)
            if n < 3:
                if n + 1 in OPT["DV"]:
                    ts(v("dd", a, b), v("cp", a, b), 1.0, A.is_gt, 2.0, A.mult)
                else:
                    act(v("dd", a, b), v("cp", a, b), F.Sign, 1.0, -1.0)
                act(v("rr", a, b), v("cp", a, b), F.Sign, -1.0, -2.0 ** -60)
                tag("r", n)
        if n < 3:
            act(v("sc%d" % n, 0, 96), ind(v("cp", 0, L), lu), F.Copy, 0.5)
            sent["c"] = send("sc%d" % n, "lc%d" % n, "rc%d" % n)
        masked, wide = n in OPT["FM"], 2.0 ** (n + 1)
        for k, (a, b) in enumerate(CH):
            dh = ind(v("dt", 0, H + 16), lst(fi, a, b))
            if masked:
                o = mm(P(5 + k % 2, 0, b - a), [(Iw[n], act(v("db", a, b), dh, F.Copy)), (FN, v(cr, a, b))])
                act(v("ff", a, b), o, F.Sigmoid, wide)
            else:
                act(v("ff", a, b), dh, F.Sigmoid)
            tag("f", n)
            if n == 1 and k == 0:
                ops[-1]["cost"] += 1.3
                ops[-1]["hold"] += 1.3
            tt(v("aq", a, b), ind(v("wa", 0, NA) if n > 1 else v("amb", 0, ARR), lst(ia, a, b)), v("ff", a, b), A.mult)
            tag("a", n)
        src, twin = ("aq", "ar") if masked else (cq, cr)
        if not masked:
            move("g", v(cq, 0, L), v("aq", 0, L), True)
        for k, (a, b) in enumerate(CH):
            copy(OPT["A2"][n - 1][k], v(twin, a, b), v(src, a, b))
            tt(v("wa", PAD + a, PAD + b), ind(v(src, 0, L + 192 * (n in OPT["AP"])), lst(i2a, a, b)), v(twin, a, b), A.max if masked else A.min)
            tag("b", n)
        if n < 3:
            act(v("sa%d" % n, 0, 96), ind(v("wa", PAD, ARR), lu), F.Copy)
            sent["a"] = send("sa%d" % n, "la%d" % n, "ra%d" % n)
    for k, (a, b) in enumerate(CH):
        tt(v("oa", a, b), ind(v("kt", 0, PAD + H), lst(hu, a, b)), v("wa", PAD + a, PAD + b), A.mult)
        dma("y", T.ya[:, a:b], T.oa[:, a:b], [v("oa", a, b)], [], 4 * (b - a))
        o = mm(P(5 + k % 2, 0, b - a), [(I20, act(v("dd", a, b), v("oa", a, b), F.Sign))])
        tt(v("oc", a, b), v("cp", a, b), o, A.mult)
        dma("y", T.yc[:, a:b], T.oc[:, a:b], [v("oc", a, b)], [], 4 * (b - a))

    no = len(ops)
    succ = [[] for _ in range(no)]
    for i, o in enumerate(ops):
        o["pre"] = [(j, LAT) for j in o["deps"]] + ([(o["after"], NET)] if o["after"] is not None else [])
    for a, b in OPT["HINT"]:
        for i in tags[b]:
            ops[i]["pre"] += [(j, 0.0) for j in tags[a]]
    for i, o in enumerate(ops):
        for j, lat in o["pre"]:
            succ[j].append((i, lat))
    pred = [o["pre"] for o in ops]
    cost = [o["cost"] for o in ops]
    use = []
    for o in ops:
        use.append([(o["e"], 0.0, o["hold"], None)] + [(b, 0.0, o["cost"] + LAT, o["e"]) for b in o["banks"]])
        if o["bw"]:
            use[-1].append(("dma", o["cost"] - o["bw"] - 0.5, o["bw"], None))
    back = [[(r, cost[i] - a - d, d, e) for r, a, d, e in use[i]] for i in range(no)]

    def place(seq, before, uses):
        start, busy = [0.0] * no, {}
        for i in seq:
            t0 = max([start[j] + cost[j] + lat for j, lat in before[i]], default=0.0)
            moved = True
            while moved:
                moved = False
                for r, a, d, e in uses[i]:
                    lane = busy.setdefault(r, [])
                    k = len(lane)
                    while k and lane[k - 1][1] > t0 + a - 3.0:
                        k -= 1
                    for x, y, e2 in lane[k:]:
                        if x >= t0 + a + d - 1e-9:
                            break
                        if y > t0 + a + 1e-9 and (e is None or e != e2):
                            t0, moved = y - a, True
            for r, a, d, e in uses[i]:
                lane = busy[r]
                k = len(lane)
                while k and lane[k - 1][0] > t0 + a:
                    k -= 1
                lane.insert(k, (t0 + a, t0 + a + d, e))
            start[i] = t0
        return start, max(start[i] + cost[i] for i in range(no))

    def ranked(pr, before, behind):
        left, out = [len(x) for x in before], []
        cand = [i for i in range(no) if left[i] == 0]
        while cand:
            i = max(cand, key=lambda j: pr[j])
            cand.remove(i)
            out.append(i)
            for j, lat in behind[i]:
                left[j] -= 1
                if left[j] == 0:
                    cand.append(j)
        return out

    key = str(sorted(OPT.items())) + str((CY, GC, SC, LAT, PC, DM, NET, OV, BW, GH))
    if key not in KEPT:
        seed, prio, cur, best = [OPT["SEED"]], [-float(i) for i in range(no)], None, None

        def rnd():
            seed[0] = (seed[0] * 1103515245 + 12345) % 2147483648
            return seed[0] / 2147483648

        for it in range(OPT["IT"]):
            start, end = place(ranked(prio, pred, succ), pred, use)
            aim = end + OPT["MW"] * sum(start[i] for n in "123" for i in tags["x" + n])
            if cur is None or aim < cur[0] + OPT["AL"] * (1 - it / OPT["IT"]) * rnd():
                cur = (aim, start)
            if best is None or end < best[0]:
                best = (end, start)
            fin = [cur[1][i] + cost[i] + OPT["NZ"] * rnd() for i in range(no)]
            for _ in range(OPT["KICK"]):
                a, w, s = int(rnd() * no), int(rnd() ** 2 * 40) + 1, (rnd() - 0.5) * OPT["KW"]
                e = ops[a]["e"] if rnd() < 0.5 else None
                for i in range(a, min(no, a + w)):
                    if e in (None, ops[i]["e"]):
                        fin[i] += s
            rstart = place(ranked(fin, succ, pred), succ, back)[0]
            prio = [rstart[i] + cost[i] for i in range(no)]
        seq = sorted(range(no), key=lambda i: (best[1][i], i))
        eng, hold = [o["e"] for o in ops], [o["hold"] for o in ops]
        banks, bw = [o["banks"] for o in ops], [o["bw"] for o in ops]
        marks = [tags["x" + n][0] for n in "123"]

        cases = []
        for fe, fd in OPT["CASES"]:
            cases.append(([c * (fd if o["sem"] else fe) for c, o in zip(cost, ops)],
                          [h * (fd if o["sem"] else fe) for h, o in zip(hold, ops)], [x * fd for x in bw],
                          [[(j, lat * (fd if lat == NET else 1)) for j, lat in x] for x in pred]))

        def timed(seq):
            out = [timed1(seq, *c) for c in cases]
            pick = out[int(rnd() * len(out))]
            n = len(out)
            return sum(x[0] for x in out) / n, sum(x[1] for x in out) / n, pick[2], pick[3], pick[4]

        def timed1(seq, cost, hold, bw, pred):
            fin, start, why, busy, turn, lane = [0.0] * no, [0.0] * no, [None] * no, {}, {}, (0.0, None)
            for i in seq:
                e = eng[i]
                t0, w = busy.get(e, (0.0, None))
                for j, lat in pred[i]:
                    if fin[j] + lat > t0:
                        t0, w = fin[j] + lat, ~j
                for b in banks[i]:
                    x = turn.get(b)
                    if x:
                        f, j = x[0] if x[2] != e else x[1]
                        if f > t0:
                            t0, w = f, j
                f = t0 + cost[i]
                if bw[i]:
                    if lane[0] + bw[i] + 0.5 > f:
                        f, w = lane[0] + bw[i] + 0.5, lane[1]
                    lane = (f - 0.5, i)
                for b in banks[i]:
                    x = turn.get(b)
                    turn[b] = ((f + LAT, i), (x[0] if x[2] != e else x[1]) if x else (0.0, None), e)
                busy[e], fin[i], start[i], why[i] = (t0 + hold[i], i), f, t0, w
            end = max(fin)
            return end + OPT["MW"] * sum(start[i] for i in marks), end, start, why, fin.index(end)

        def moved(seq, a, b, up):
            part = seq[a:b + 1]
            if up:
                part.reverse()
            need, go, rest = {part[0]}, [], []
            for k in part:
                if k in need:
                    go.append(k)
                    need.update(x for x, lat in (pred if up else succ)[k])
                else:
                    rest.append(k)
            part = go[::-1] + rest[::-1] if up else rest + go
            return seq[:a] + part + seq[b + 1:]

        cur = timed(seq)
        best = (cur[1], seq, cur[2])
        for it in range(OPT["LS"]):
            i, held = cur[4] if rnd() > OPT["LM"] else marks[int(rnd() * 3)], []
            while cur[3][i] is not None:
                j = cur[3][i]
                if j >= 0:
                    held.append((j, i))
                i = j if j >= 0 else ~j
            if held and rnd() < OPT["LC"]:
                j, i = held[int(rnd() * len(held))]
                a, b = max(0, seq.index(j) - int(rnd() ** 3 * OPT["LW"])), seq.index(i)
            else:
                a = int(rnd() * (no - 1))
                b = min(no - 1, a + 1 + int(rnd() ** 2 * 2 * OPT["LW"]))
            s2 = moved(seq, a, b, rnd() < 0.5)
            c2 = timed(s2)
            if c2[0] <= cur[0] + OPT["LT"] * (1 - it / OPT["LS"]) * rnd() ** 2:
                seq, cur = s2, c2
                if cur[1] < best[0]:
                    best = (cur[1], seq, cur[2])
        KEPT[key] = best
    order = KEPT[key][1]
    for i in range(no):
        ops[i]["t"] = KEPT[key][2][i]
    last = {}
    for i in order:
        for b in ops[i]["banks"]:
            ops[i]["deps"].update(j for e, j in last.setdefault(b, {}).items() if e != ops[i]["e"])
            last[b][ops[i]["e"]] = i
        if ops[i]["scatter"]:
            ops[i]["deps"].update(last.get("scatter", []))
            last["scatter"] = [i]

    queue = {"v": g.vector, "s": g.scalar, "p": g.tensor, "g": g, "y": g.sync}
    esem = {"v": "sv", "s": "ss", "p": "sp", "g": "sg"}
    count = {}
    known = {e: {} for e in queue}
    for i in order:
        o = ops[i]
        e = o["e"]
        need = {}
        for j in o["deps"]:
            p = ops[j]
            if p["mark"] is None or (e == "p" and p["e"] == "p"):
                continue
            s, c = p["mark"]
            if known[e].get(s, 0) < c and need.get(s, (0, 0))[0] < c:
                need[s] = (c, j)
        for s, (c, j) in sorted(need.items(), key=lambda kv: -ops[kv[1][1]]["t"]):
            if known[e].get(s, 0) < c:
                queue[e].wait_ge(T.sem[s], c)
                for s2, c2 in ops[j]["clock"].items():
                    known[e][s2] = max(known[e].get(s2, 0), c2)
        if o["xw"] is not None and known[e].get(o["xw"][0], 0) < o["xw"][1]:
            queue[e].wait_ge(T.sem[o["xw"][0]], o["xw"][1])
            known[e][o["xw"][0]] = o["xw"][1]
        ins = o["fn"]()
        if o["sem"] == "none":
            o["mark"] = None
            continue
        s, inc = (o["sem"], 16) if o["sem"] else (esem[e], 1)
        count[s] = count.get(s, 0) + inc
        ins.then_inc(T.sem[s], inc)
        o["mark"] = (s, count[s])
        o["clock"] = dict(known[e])
        o["clock"][s] = count[s]
    for s, c in list(count.items()) + list(names.items()):
        if known["g"].get(s, 0) < c:
            g.wait_ge(T.sem[s], c)
